import numpy as np, ml_dtypes
CORES = [66,74,82,90,194,202,210,218]
N = 8
import mx_ref
BF = ml_dtypes.bfloat16
def entries(a):
    return np.ascontiguousarray(a.T).reshape(-1)
def table(e):
    return np.ascontiguousarray(np.reshape(e, (-1, 16)).T).astype(np.int32)
def cols(t, e):
    v = np.concatenate([t.reshape(128, -1, 4), np.zeros((128, 1, 4), BF)], axis=1)
    return np.ascontiguousarray(v[:, e]).reshape(128, -1)
def f(rng, *shape):
    return mx_ref.flush((rng.standard_normal(shape, dtype=np.float32) * np.exp2(rng.integers(-2, 3, shape[:-1] + (1,)))).astype(BF))
def wide(rng, *shape, cols=0):
    v = rng.standard_normal(shape, dtype=np.float32) * np.exp2(rng.integers(-12, 13, shape)).astype(np.float32)
    if cols: v *= np.repeat(np.exp2(rng.integers(-cols, cols + 1, shape[:-2] + (1, shape[-1] // 4))) * (rng.random(shape[:-2] + (1, shape[-1] // 4)) > 0.0625), 4, axis=-1).astype(np.float32)
    return mx_ref.flush(v.astype(BF))
TA, TB, CI, CJ, JW = 256, 256, 32, 48, 384
SIDE = [0 if c < 128 else 1 for c in CORES]
GCOL = [SIDE[:r].count(SIDE[r]) for r in range(N)]
def fill(rng, total, cap, wd, first, back):
    n = np.zeros(N, int)
    for q in first: n[q] = min(cap, total - n.sum())
    while n.sum() < total:
        q = rng.integers(0, N)
        if n[q] < cap: n[q] += 1
    s, used = np.full((N, cap), -1), []
    for q in range(N):
        k, v = rng.permutation(cap)[:n[q]], rng.integers(0, wd, n[q])
        if back: k, v = np.sort(k), np.sort(v)[::-1]
        s[q, k] = v; used += list(q * cap + k)
    return s, (np.sort(used)[::-1] if back else rng.permutation(used))
def lists(rng, full=False, own=False, back=False, alike=False):
    A, B = [], []
    for i in range(2):
        A.append(fill(rng, 128, CI, TA, rng.permutation(N) if full else [r for r in range(N) if own and SIDE[r] == i], back))
    for k in range(4):
        B.append(fill(rng, JW, CJ, TB, rng.permutation(N) if full else [r for r in range(N) if own and GCOL[r] == k], back))
    if alike: B = [B[0]] * 4
    return {"sa": np.stack([table(np.concatenate([A[i][0][q] for i in range(2)])) for q in range(N)]),
            "sb": np.stack([table(np.concatenate([B[k][0][q] for k in range(4)])) for q in range(N)]),
            "pi": np.stack([table(A[SIDE[r]][1]) for r in range(N)]), "pj": np.stack([table(B[GCOL[r]][1]) for r in range(N)])}
def setup_inputs(rng):
    return {"a": f(rng, N, 128, 4 * TA), "b": f(rng, N, 128, 4 * TB), **lists(rng)}
def setup_inputs_alike(rng):
    return {**setup_inputs(rng), **lists(rng, alike=True)}
def setup_inputs_full(rng):
    return {**setup_inputs(rng), **lists(rng, full=True)}
def setup_inputs_own(rng):
    return {**setup_inputs(rng), **lists(rng, own=True)}
def setup_inputs_reversed(rng):
    return {**setup_inputs(rng), **lists(rng, back=True)}
def setup_inputs_spread(rng):
    d = setup_inputs(rng); d["a"], d["b"] = wide(rng, N, 128, 4 * TA, cols=6), wide(rng, N, 128, 4 * TB, cols=6); return d
def check_inputs(d):
    bad = []
    for s, p, wd, cap, total, place in (("sa", "pi", TA, CI, 128, SIDE), ("sb", "pj", TB, CJ, JW, GCOL)):
        e = np.stack([entries(d[s][q]) for q in range(N)])
        if e.min() < -1 or e.max() >= wd: bad.append(s)
        for r in range(N):
            v = e[:, cap * place[r]:cap * place[r] + cap].reshape(-1)
            if (v >= 0).sum() != total: bad.append(s + " count")
            t = entries(d[p][r])
            if t.min() < 0 or t.max() >= N * cap: bad.append(p); continue
            if len(set(t.tolist())) != total or (v[t] < 0).any(): bad.append(p + " slots")
            if (d[p][r] != d[p][place.index(place[r])]).any(): bad.append(p + " not the same")
    return bad
def reference(a, b, sa, sb, pi, pj):
    y = np.zeros((N, 128, JW), np.float32)
    for r in range(N):
        i, k = SIDE[r], GCOL[r]
        A = np.concatenate([cols(a[q], entries(sa[q])[CI * i:CI * i + CI]) for q in range(N)], axis=1)
        B = np.concatenate([cols(b[q], entries(sb[q])[CJ * k:CJ * k + CJ]) for q in range(N)], axis=1)
        y[r] = mx_ref.matmul(mx_ref.quantize(cols(A, entries(pi[r]))), mx_ref.quantize(cols(B, entries(pj[r]))))
    return {"y": y}

@@ -1,0 +1,252 @@
+from concourse.bass import DstId, RemoteDMATransfer
+from concourse.mybir import dt, AluOpType, ActivationFunctionType
+
+N, NC, CI, CJ, JW = 8, 4, 32, 48, 384
+HB = NC * CJ
+TW = 160
+
+SCRATCH = {
+    "abuf": ("sbuf", [128, 1024], "bfloat16"),
+    "bbuf": ("sbuf", [128, 1024], "bfloat16"),
+    "lst": ("sbuf", [32, 16], "int32"),
+    "l4": ("sbuf", [128, 16], "int32"),
+    "off": ("sbuf", [128, 64], "uint16"),
+    "ta": ("sbuf", [128, 4 * TW], "bfloat16"),
+    "tb": ("sbuf", [128, 4 * HB], "bfloat16"),
+    "cac": ("sbuf", [128, TW], "float8_e4m3fn_x4"),
+    "cas": ("sbuf", [128, TW], "uint8"),
+    "cbc": ("sbuf", [128, HB], "float8_e4m3fn_x4"),
+    "cbs": ("sbuf", [128, HB], "uint8"),
+    "hxc": ("sbuf", [128, CI], "float8_e4m3fn_x4"),
+    "hys": ("sbuf", [128, 256], "uint8"),
+    "lac": ("sbuf", [128, 256], "float8_e4m3fn_x4"),
+    "las": ("sbuf", [128, 256], "uint8"),
+    "lbc": ("sbuf", [128, JW], "float8_e4m3fn_x4"),
+    "lbs": ("sbuf", [128, JW], "uint8"),
+    "ps": ("psum", [128, 2048], "float32"),
+    "prod": ("sbuf", [128, 768], "float32"),
+    "pick0": ("sbuf", [128, 192], "float32"),
+    "pick1": ("sbuf", [128, 192], "float32"),
+    "turned": ("sbuf", [128, 192], "float32"),
+    "fin": ("sbuf", [128, JW], "float32"),
+    "yout": ("sbuf", [128, JW], "float32"),
+    "lq": ("sbuf", [32, 32], "int32"),
+    "k1": ("sbuf", [32, 32], "int32"),
+    "k2": ("sbuf", [32, 32], "int32"),
+    "k3": ("sbuf", [32, 32], "int32"),
+    "k4": ("sbuf", [32, 32], "int32"),
+    "k5": ("sbuf", [32, 32], "int32"),
+    "ix": ("sbuf", [32, 48], "int32"),
+    "ixu": ("sbuf", [128, 48], "uint16"),
+}
+SEMAPHORES = ["la", "lb", "ll", "lp", "vz", "v1", "v2", "gav", "gas", "qa", "gbv", "gbs", "qb", "vx",
+              "oc", "hx", "hy", "aa", "b1c", "b1s", "b2", "ls", "m0", "m1", "m2", "m3",
+              "cp", "g0", "g1", "tt", "ft", "out", "st"]
+COPY = ActivationFunctionType.Copy
+
+
+def bits(engines):
+    m = 0
+    for e in engines:
+        m |= 1 << e
+    return m
+
+
+def move(topo, core, dsts, src, dst, engines, sem):
+    ids = []
+    for d in dsts:
+        rid, pid = topo.addr(d, core)
+        ids.append(DstId(rid=rid, pnc=pid))
+    return RemoteDMATransfer(dst_ids=ids, srcs=[src], dsts=[dst] * len(ids), dma_engine_mask=bits(engines), remote_sem=sem)
+
+
+def forwarders(topo, rank_core, side):
+    ok = [c for c in topo.cores_of(rank_core) if c != rank_core and all(topo.may_write(c, d) for d in side)]
+    ok = [c for c in ok if topo.die(c) == topo.die(rank_core)] + [c for c in ok if topo.die(c) != topo.die(rank_core)]
+    return ok[:3]
+
+
+def rank_program(g, core, T, topo):
+    cores = list(T.cores)
+    sides = [[c for c in cores if topo.host(c) == topo.host(cores[0])], [c for c in cores if topo.host(c) != topo.host(cores[0])]]
+    if T.rank_of(core) is None:
+        for h in range(2):
+            for c in range(NC):
+                fw = forwarders(topo, sides[h][c], sides[h])
+                if core in fw:
+                    forward(g, core, T, topo, sides, h, c, fw.index(core))
+        return
+    h = 0 if core in sides[0] else 1
+    rank_core(g, core, T, topo, sides, h, sides[h].index(core))
+
+
+def a_plan(topo, me, fx, gx):
+    off = topo.engines(me, gx)
+    on = [e for e in topo.engines(me, fx) if e not in off]
+    return off[:4], off[4:8], on[:2], on[2:4]
+
+
+def forward(g, core, T, topo, sides, h, c, role):
+    engines = topo.engines(core, sides[h][0])
+    for d in sides[h]:
+        engines = [e for e in engines if e in topo.engines(core, d)]
+    if role < 2:
+        g.wait_ge(T.sem.hx, 2 if role == 0 else 4)
+        k = c * 64 + CI * (h if role == 0 else 1 - h)
+        tr = move(topo, core, sides[h], T.hxc[:].bitcast(dt.uint8), T.lac[:, k:k + CI].bitcast(dt.uint8), engines, T.sem.aa)
+    else:
+        g.wait_ge(T.sem.hy, 6)
+        tr = move(topo, core, sides[h], T.hys[:, 96:160], T.las[:, c * 64:c * 64 + 64], engines, T.sem.aa)
+    g.remote_dma_fused([tr], local_sem=T.sem.ls)
+    g.wait_ge(T.sem.ls, len(engines))
+
+
+def rank_core(g, me, T, topo, sides, h, c):
+    S = T.sem
+    V, A, X, Y = g.vector, g.scalar, g.tensor, g.sync
+    mine, r = sides[h], h * NC + c
+    partner = sides[1 - h][c]
+    ba = 96 if h == 0 else 0
+    own = slice(h * HB, h * HB + HB)
+
+    for i, q in ((0, Y), (1, A)):
+        q.dma_start(T.lst[16 * i:16 * i + 16, 0:4], T.sa[:]).then_inc(S.ll, 16)
+        q.dma_start(T.lst[16 * i:16 * i + 16, 4:16], T.sb[:]).then_inc(S.ll, 16)
+    Y.dma_start(T.abuf[:], T.a[:]).then_inc(S.la, 16)
+    Y.dma_start(T.bbuf[:], T.b[:]).then_inc(S.lb, 16)
+    for i in range(2):
+        A.dma_start(T.lq[16 * i:16 * i + 16, 0:24], T.pj[:]).then_inc(S.lp, 16)
+        A.dma_start(T.lq[16 * i:16 * i + 16, 24:32], T.pi[:]).then_inc(S.lp, 16)
+
+    V.memset(T.ta[:, (0 if h == 0 else 4 * 64):(4 * 96 if h == 0 else 4 * TW)], 0.0).then_inc(S.vz, 1)
+    V.wait_ge(S.ll, 64)
+    for b in range(4):
+        V.tensor_scalar(T.l4[32 * b:32 * b + 32, :], T.lst[:], 4, 0, AluOpType.mult, AluOpType.max).then_inc(S.v1, 1)
+    V.wait_ge(S.v1, 4)
+    for t in range(4):
+        V.tensor_scalar(T.off[:, 16 * t:16 * t + 16], T.l4[:], t, None, AluOpType.add).then_inc(S.v2, 1)
+    V.wait_ge(S.v2, 4)
+    A.wait_ge(S.v2, 4)
+    V.wait_ge(S.la, 16)
+    A.wait_ge(S.la, 16)
+
+    def pick(t, tile, first, n, win, o, sem):
+        out, in_ = tile[:, 4 * first + t:4 * (first + n):4], win[:, 0:1024].indirect(T.off[:, 16 * t + o:16 * t + o + n // 16])
+        if t < 2:
+            V.tensor_copy(out, in_).then_inc(sem, 1)
+        else:
+            A.activation(out, in_, COPY).then_inc(sem, 1)
+
+    for t in range(4):
+        pick(t, T.ta, ba, 2 * CI, T.abuf, 0, S.gav if t < 2 else S.gas)
+    V.wait_ge(S.vz, 1)
+    V.wait_ge(S.gav, 2)
+    V.wait_ge(S.gas, 2)
+    V.quantize_mx(T.cac[:], T.cas[:], T.ta[:]).then_inc(S.qa, 1)
+    V.wait_ge(S.lb, 16)
+    A.wait_ge(S.lb, 16)
+    for t in range(4):
+        pick(t, T.tb, 0, HB, T.bbuf, 4, S.gbv if t < 2 else S.gbs)
+    V.wait_ge(S.gbv, 2)
+    V.wait_ge(S.gbs, 2)
+    V.quantize_mx(T.cbc[:], T.cbs[:], T.tb[:]).then_inc(S.qb, 1)
+
+    Y.wait_ge(S.qb, 1)
+    Y.dma_start(T.lbc[:, r * CJ:r * CJ + CJ].bitcast(dt.uint8), T.cbc[:, c * CJ:c * CJ + CJ].bitcast(dt.uint8)).then_inc(S.oc, 16)
+    Y.dma_start(T.lbs[:, r * CJ:r * CJ + CJ], T.cbs[:, c * CJ:c * CJ + CJ]).then_inc(S.oc, 16)
+
+    fo, _fp, fs = forwarders(topo, me, mine)
+    _go, gp, gs = forwarders(topo, partner, sides[1 - h])
+    e1, e2, e3, e4 = a_plan(topo, me, fo, gp)
+    ls = len(e1) + len(e2) + len(e3) + len(e4)
+    g.wait_ge(S.qa, 1)
+    tr = []
+    for s, cx, cy, ex, ey in ((1 - h, gp, gs, e1, e2), (h, fo, fs, e3, e4)):
+        k = ba + CI * s
+        tr.append(move(topo, me, [cx], T.cac[:, k:k + CI].bitcast(dt.uint8), T.hxc[:].bitcast(dt.uint8), ex, S.hx))
+        tr.append(move(topo, me, [cy], T.cas[:, CI * s:CI * s + 128], T.hys[:, 128 * h:128 * h + 128], ey, S.hy))
+    g.remote_dma_fused(tr, local_sem=S.ls)
+
+    peers = [d for d in mine if d != me]
+    peers = [d for d in peers if not topo.mates(me, d) and not topo.same_plane(me, d)] + \
+            [d for d in peers if topo.mates(me, d) or topo.same_plane(me, d)]
+    off = topo.engines(me, peers[0])
+    g.wait_ge(S.qb, 1)
+    trc, trs = [], []
+    for i, d in enumerate(peers):
+        ec = off[0:4] if i == 0 else off[4 + 2 * i - 2:4 + 2 * i]
+        es = off[4:8] if i == 0 else off[2 * i - 2:2 * i]
+        k = mine.index(d)
+        trc.append(move(topo, me, [d], T.cbc[:, k * CJ:k * CJ + CJ].bitcast(dt.uint8), T.lbc[:, r * CJ:r * CJ + CJ].bitcast(dt.uint8), ec, S.b1c))
+        trs.append(move(topo, me, [d], T.cbs[:, k * CJ:k * CJ + CJ], T.lbs[:, r * CJ:r * CJ + CJ], es, S.b1s))
+    g.remote_dma_fused(trc, local_sem=S.ls)
+    g.remote_dma_fused(trs, local_sem=S.ls)
+    ls += 16
+
+    rid, pid = topo.addr(partner, me)
+    m = bits(topo.engines(me, partner))
+    g.wait_ge(S.oc, 32)
+    g.wait_ge(S.b1c, 8)
+    g.remote_dma(T.lbc[:, own].bitcast(dt.uint8), T.lbc[:, own].bitcast(dt.uint8), S.b2, S.ls, pid, rid, m)
+    g.wait_ge(S.b1s, 8)
+    g.remote_dma(T.lbs[:, own], T.lbs[:, own], S.b2, S.ls, pid, rid, m)
+    ls += 2 * len(topo.engines(me, partner))
+    g.wait_ge(S.ls, ls)
+
+    V.wait_ge(S.lp, 64)
+    V.tensor_scalar(T.k1[:], T.lq[:], 96, None, AluOpType.bitwise_and).then_inc(S.vx, 1)
+    V.tensor_scalar(T.k2[:], T.lq[:], 384, None, AluOpType.bitwise_and).then_inc(S.vx, 1)
+    V.wait_ge(S.vx, 2)
+    V.tensor_scalar(T.k3[:], T.k2[:], -0.75, None, AluOpType.mult).then_inc(S.vx, 1)
+    V.wait_ge(S.vx, 3)
+    V.tensor_tensor(T.k4[:], T.lq[:], T.k3[:], AluOpType.add).then_inc(S.vx, 1)
+    V.wait_ge(S.vx, 4)
+    V.tensor_tensor(T.k5[:], T.k4[:], T.k1[:], AluOpType.add).then_inc(S.vx, 1)
+    V.wait_ge(S.vx, 5)
+    V.tensor_tensor(T.ix[:, 0:24], T.k5[:, 0:24], T.k1[:, 0:24], AluOpType.add).then_inc(S.vx, 1)
+    for t in range(3):
+        for u in range(2):
+            V.tensor_scalar(T.ix[:, 24 + 2 * t + u:48:6], T.k5[:, 24 + u:32:2], 256 * t, None, AluOpType.add).then_inc(S.vx, 1)
+    V.wait_ge(S.vx, 12)
+    for b in range(4):
+        V.tensor_copy(T.ixu[32 * b:32 * b + 32, :], T.ix[:]).then_inc(S.vx, 1)
+    V.wait_ge(S.vx, 16)
+    A.wait_ge(S.vx, 16)
+
+    e, l = (0, 1) if h == 0 else (2, 0)
+    X.wait_ge(S.oc, 32)
+    X.wait_ge(S.b1c, 8)
+    X.wait_ge(S.b1s, 8)
+    X.wait_ge(S.aa, 96)
+    for bank, t, x, w in ((0, e, 0, 256), (1, l, 0, 256), (2, l + 1, 0, 128), (3, l + 1, 128, 128)):
+        if bank == 1:
+            X.wait_ge(S.b2, 2 * len(topo.engines(partner, me)))
+        X.matmul_mx(T.ps[:, 512 * bank:512 * bank + w], T.lbc[:, 128 * t:128 * t + 128], T.lbs[:, 128 * t:128 * t + 128],
+                    T.lac[:, x:x + w], T.las[:, x:x + w], True, True).then_inc(S["m%d" % bank], 1)
+        A_or_V = A.activation if bank in (0, 2) else V.tensor_copy
+        (A if bank in (0, 2) else V).wait_ge(S["m%d" % bank], 1)
+        args = (T.prod[:, 256 * t + x:256 * t + x + w], T.ps[:, 512 * bank:512 * bank + w])
+        (A_or_V(*args, COPY) if bank in (0, 2) else A_or_V(*args)).then_inc(S.cp, 1)
+
+    for q in (V, A):
+        q.wait_ge(S.cp, 4)
+    win = T.prod[:, 0:768]
+    V.tensor_copy(T.pick1[:], win.indirect(T.ixu[:, 36:48])).then_inc(S.g1, 1)
+    A.activation(T.pick0[:], win.indirect(T.ixu[:, 24:36]), COPY).then_inc(S.g0, 1)
+    V.wait_ge(S.g1, 1)
+    V.transpose(T.turned[:], T.pick1[:]).then_inc(S.tt, 1)
+    A.wait_ge(S.tt, 1)
+    V.wait_ge(S.g0, 1)
+    for b in range(2):
+        for a in range(4):
+            V.transpose(T.fin[32 * b:32 * b + 32, 96 * a:96 * a + 96], T.pick0[32 * a:32 * a + 32, 96 * b:96 * b + 96]).then_inc(S.ft, 1)
+            A.activation(T.fin[32 * b + 64:32 * b + 96, 96 * a:96 * a + 96], T.turned[32 * a:32 * a + 32, 96 * b:96 * b + 96],
+                         COPY).then_inc(S.ft, 1)
+
+    for q in (V, A):
+        q.wait_ge(S.ft, 16)
+    V.tensor_copy(T.yout[:, 0:192], T.fin[:, 0:JW].indirect(T.ixu[:, 0:12])).then_inc(S.out, 1)
+    A.activation(T.yout[:, 192:JW], T.fin[:, 0:JW].indirect(T.ixu[:, 12:24]), COPY).then_inc(S.out, 1)
+    Y.wait_ge(S.out, 2)
+    Y.dma_start(T.y[:], T.yout[:]).then_inc(S.st, 16)
+    Y.wait_ge(S.st, 16)

@@ -4,249 +4,298 @@ from concourse.mybir import dt, AluOpType, ActivationFunctionType
 N, NC, CI, CJ, JW = 8, 4, 32, 48, 384
 HB = NC * CJ
 TW = 160
+LB = HB - CJ
+PAD = 16
 
 SCRATCH = {
-    "abuf": ("sbuf", [128, 1024], "bfloat16"),
-    "bbuf": ("sbuf", [128, 1024], "bfloat16"),
-    "lst": ("sbuf", [32, 16], "int32"),
-    "l4": ("sbuf", [128, 16], "int32"),
-    "off": ("sbuf", [128, 64], "uint16"),
+    "abuf": ("sbuf", [128, PAD + 1024], "bfloat16"),
+    "bbuf": ("sbuf", [128, PAD + 1024], "bfloat16"),
+    "lst": ("sbuf", [128, 4, 6], "int32"),
+    "off": ("sbuf", [128, 72], "uint16"),
     "ta": ("sbuf", [128, 4 * TW], "bfloat16"),
     "tb": ("sbuf", [128, 4 * HB], "bfloat16"),
-    "cac": ("sbuf", [128, TW], "float8_e4m3fn_x4"),
+    "ac": ("sbuf", [128, 384], "float8_e4m3fn_x4"),
     "cas": ("sbuf", [128, TW], "uint8"),
-    "cbc": ("sbuf", [128, HB], "float8_e4m3fn_x4"),
-    "cbs": ("sbuf", [128, HB], "uint8"),
-    "hxc": ("sbuf", [128, CI], "float8_e4m3fn_x4"),
-    "hys": ("sbuf", [128, 256], "uint8"),
-    "lac": ("sbuf", [128, 256], "float8_e4m3fn_x4"),
     "las": ("sbuf", [128, 256], "uint8"),
-    "lbc": ("sbuf", [128, JW], "float8_e4m3fn_x4"),
-    "lbs": ("sbuf", [128, JW], "uint8"),
+    "bc": ("sbuf", [128, LB + JW], "float8_e4m3fn_x4"),
+    "bs": ("sbuf", [128, LB + JW], "uint8"),
+    "hc": ("sbuf", [128, CJ], "float8_e4m3fn_x4"),
+    "hs": ("sbuf", [128, 256], "uint8"),
     "ps": ("psum", [128, 2048], "float32"),
     "prod": ("sbuf", [128, 768], "float32"),
-    "pick0": ("sbuf", [128, 192], "float32"),
-    "pick1": ("sbuf", [128, 192], "float32"),
+    "pick": ("sbuf", [128, JW], "float32"),
     "turned": ("sbuf", [128, 192], "float32"),
     "fin": ("sbuf", [128, JW], "float32"),
     "yout": ("sbuf", [128, JW], "float32"),
-    "lq": ("sbuf", [32, 32], "int32"),
-    "k1": ("sbuf", [32, 32], "int32"),
-    "k2": ("sbuf", [32, 32], "int32"),
-    "k3": ("sbuf", [32, 32], "int32"),
-    "k4": ("sbuf", [32, 32], "int32"),
-    "k5": ("sbuf", [32, 32], "int32"),
-    "ix": ("sbuf", [32, 48], "int32"),
+    "lq": ("sbuf", [128, 32], "int32"),
+    "k1": ("sbuf", [128, 32], "int32"),
+    "k2": ("sbuf", [128, 32], "int32"),
+    "k3": ("sbuf", [128, 32], "int32"),
+    "k4": ("sbuf", [128, 32], "int32"),
+    "k5": ("sbuf", [128, 32], "int32"),
+    "k6": ("sbuf", [128, 32], "int32"),
+    "ext": ("sbuf", [128, 48], "int32"),
     "ixu": ("sbuf", [128, 48], "uint16"),
 }
-SEMAPHORES = ["la", "lb", "ll", "lp", "vz", "v1", "v2", "gav", "gas", "qa", "gbv", "gbs", "qb", "vx",
-              "oc", "hx", "hy", "aa", "b1c", "b1s", "b2", "ls", "m0", "m1", "m2", "m3",
-              "cp", "g0", "g1", "tt", "ft", "out", "st"]
+CODES = ("ac", "bc", "hc")
+SEMAPHORES = ["la", "lb", "ll", "lp", "vz", "v1", "v2", "v3", "gav", "gas", "qa", "gbv", "gbs", "qb", "vx",
+              "hx", "aa", "b1", "b2", "b3", "bb", "ls", "m0", "m1", "m2", "m3",
+              "cp", "g0", "g1", "t2", "t3", "ft", "o0", "o1", "st"]
 COPY = ActivationFunctionType.Copy
 
 
-def bits(engines):
-    m = 0
-    for e in engines:
-        m |= 1 << e
-    return m
+def helpers(topo, rank_core, side):
+    rest = [c for c in topo.cores_of(rank_core) if c != rank_core]
+    rest = [c for c in rest if topo.die(c) == topo.die(rank_core)] + [c for c in rest if topo.die(c) != topo.die(rank_core)]
+    wide = [c for c in rest if all(topo.may_write(c, d) for d in side)]
+    return wide, [c for c in rest if c not in wide]
 
 
-def move(topo, core, dsts, src, dst, engines, sem):
-    ids = []
-    for d in dsts:
-        rid, pid = topo.addr(d, core)
-        ids.append(DstId(rid=rid, pnc=pid))
-    return RemoteDMATransfer(dst_ids=ids, srcs=[src], dsts=[dst] * len(ids), dma_engine_mask=bits(engines), remote_sem=sem)
+def a_at(h, c, h2, c2):
+    return 64 * ((c2 - c - 1 + h) % NC) + CI * (1 - h2)
 
 
-def forwarders(topo, rank_core, side):
-    ok = [c for c in topo.cores_of(rank_core) if c != rank_core and all(topo.may_write(c, d) for d in side)]
-    ok = [c for c in ok if topo.die(c) == topo.die(rank_core)] + [c for c in ok if topo.die(c) != topo.die(rank_core)]
-    return ok[:3]
+def b_run(c):
+    return LB * (c % 2)
+
+
+def b_at(h, c, h2, c2):
+    if c % 2:
+        return LB + CJ * ((c2 - c) % NC) + HB * (h != h2)
+    return CJ * ((c2 - c - 1) % NC) + HB * (h == h2)
+
+
+def b_tile(c, k):
+    return (JW - CJ) * (1 - c % 2) + CJ * ((k + 2 * (c in (1, 2))) % NC)
+
+
+def plan(topo, sides):
+    calls = {}
+    for h in range(2):
+        for c in range(NC):
+            me, mine, far_side = sides[h][c], sides[h], sides[1 - h]
+            r, partner = h * NC + c, far_side[c]
+            (fo, fp, fs), narrow = helpers(topo, me, mine)
+            (_go, gp, gs), _ = helpers(topo, partner, far_side)
+            off = topo.engines(me, partner)
+            on = [e for e in topo.engines(me, fo) if e not in off]
+            half = len(off) // 2
+            mate = [d for d in mine if topo.mates(me, d)][0]
+            near = [k for k in range(NC) if topo.same_plane(me, mine[k])][0]
+            far = [mine.index(mate)] + [k for k in range(NC) if k not in (c, near) and mine[k] != mate]
+            pc, ca = narrow[0], narrow[2]
+            pd = helpers(topo, mate, mine)[1][3]
+            peers = [k for k in range(NC) if k != c]
+            a0 = 128 * h
+            s0 = 224 if h == 0 else 96
+
+            def tile(k):
+                return b_tile(c, k)
+
+            own_run, far_run = (LB, LB + HB) if c % 2 else (HB, 0)
+
+            def one(k, buf):
+                return [(mine[k], buf, b_at(h, k, h, c))]
+
+            kd = NC - 1 - c
+            k1, k2 = [k for k in peers if k != kd]
+            kept = 2 * CJ * (c % 2)
+            calls[me] = [
+                ("qa", [("ac", s0 + CI * (1 - h), CI, [(gp, "hc", 0)], off[:half], "hx"),
+                        ("cas", CI * (1 - h), 128, [(gs, "hs", 128 * (1 - h))], off[half:], "hx"),
+                        ("ac", s0 + CI * h, CI, [(fo, "hc", 0)], on[:half], "hx"),
+                        ("cas", CI * h, 128, [(fs, "hs", 128 * (1 - h))], on[half:], "hx")]),
+                ("qb", [("bc", tile(k1), CJ, one(k1, "bc"), off[:half], "b1"),
+                        ("bc", tile(k2), CJ, one(k2, "bc"), off[half:], "b1")]),
+                (None, [("bs", tile(k1), CJ, one(k1, "bs"), off[:half], "b2"),
+                        ("bs", tile(k2), CJ, one(k2, "bs"), off[half:], "b2")]),
+                (None, [("bs", tile(kd), CJ, one(kd, "bs"), off, "b2")]),
+                (None, [("bc", tile(kd), CJ, one(kd, "bc") + [(far_side[kd], "bc", b_at(1 - h, kd, h, c))], off, "b3")]),
+                (None, [("bc", tile(c), CJ, [(partner, "bc", b_at(1 - h, c, h, c))], off, "bb")]),
+                ("b1", [("bc", own_run + kept, 2 * CJ, [(partner, "bc", far_run + kept)], off, "bb")]),
+                ("b2", [("bs", own_run, HB, [(partner, "bs", far_run)], off, "bb")]),
+            ]
+            calls[fo] = [("hx", [("hc", 0, CI, [(mine[k], "ac", a0 + a_at(h, k, h, c)) for k in peers], off, "aa")])]
+            calls[fp] = [("hx", [("hc", 0, CI, [(mine[k], "ac", a0 + a_at(h, k, 1 - h, c)) for k in peers], off, "aa"),
+                                 ("hc", 0, CI, [(me, "ac", a0 + a_at(h, c, 1 - h, c))], on[:half], "aa")])]
+            calls[fs] = [("hx", [("hs", 96, 64, [(mine[k], "las", a_at(h, k, 1, c)) for k in peers], off, "aa"),
+                                 ("hs", 96, 64, [(me, "las", a_at(h, c, 1, c))], on[:half], "aa")])]
+    return calls
+
+
+def arrivals(calls, core, sem):
+    return sum(len(t[4]) for cs in calls.values() for _w, ts in cs for t in ts for d in t[3] if d[0] == core and t[5] == sem)
+
+
+def view(T, buf, a, n):
+    v = T[buf][:, a:a + n]
+    return v.bitcast(dt.uint8) if buf in CODES else v
+
+
+def issue(g, core, T, topo, calls):
+    sent = 0
+    for wait, transfers in calls[core]:
+        if wait is not None:
+            g.wait_ge(T.sem[wait], arrivals(calls, core, wait) or 1)
+        tr = []
+        for buf, a, n, dsts, engines, sem in transfers:
+            ids = [DstId(rid=topo.addr(d, core)[0], pnc=topo.addr(d, core)[1]) for d, _b, _a in dsts]
+            tr.append(RemoteDMATransfer(dst_ids=ids, srcs=[view(T, buf, a, n)], dsts=[view(T, b, x, n) for _d, b, x in dsts],
+                                        dma_engine_mask=sum(1 << e for e in engines), remote_sem=T.sem[sem]))
+            sent += len(engines)
+        g.remote_dma_fused(tr, local_sem=T.sem.ls)
+    g.wait_ge(T.sem.ls, sent)
 
 
 def rank_program(g, core, T, topo):
     cores = list(T.cores)
     sides = [[c for c in cores if topo.host(c) == topo.host(cores[0])], [c for c in cores if topo.host(c) != topo.host(cores[0])]]
-    if T.rank_of(core) is None:
-        for h in range(2):
-            for c in range(NC):
-                fw = forwarders(topo, sides[h][c], sides[h])
-                if core in fw:
-                    forward(g, core, T, topo, sides, h, c, fw.index(core))
-        return
-    h = 0 if core in sides[0] else 1
-    rank_core(g, core, T, topo, sides, h, sides[h].index(core))
+    calls = plan(topo, sides)
+    if T.rank_of(core) is not None:
+        h = 0 if core in sides[0] else 1
+        rank_core(g, T, h, sides[h].index(core), {s: arrivals(calls, core, s) for s in ("aa", "b1", "b2", "b3", "bb")})
+    if core in calls:
+        issue(g, core, T, topo, calls)
 
 
-def a_plan(topo, me, fx, gx):
-    off = topo.engines(me, gx)
-    on = [e for e in topo.engines(me, fx) if e not in off]
-    return off[:4], off[4:8], on[:2], on[2:4]
-
-
-def forward(g, core, T, topo, sides, h, c, role):
-    engines = topo.engines(core, sides[h][0])
-    for d in sides[h]:
-        engines = [e for e in engines if e in topo.engines(core, d)]
-    if role < 2:
-        g.wait_ge(T.sem.hx, 2 if role == 0 else 4)
-        k = c * 64 + CI * (h if role == 0 else 1 - h)
-        tr = move(topo, core, sides[h], T.hxc[:].bitcast(dt.uint8), T.lac[:, k:k + CI].bitcast(dt.uint8), engines, T.sem.aa)
-    else:
-        g.wait_ge(T.sem.hy, 6)
-        tr = move(topo, core, sides[h], T.hys[:, 96:160], T.las[:, c * 64:c * 64 + 64], engines, T.sem.aa)
-    g.remote_dma_fused([tr], local_sem=T.sem.ls)
-    g.wait_ge(T.sem.ls, len(engines))
-
-
-def rank_core(g, me, T, topo, sides, h, c):
+def rank_core(g, T, h, c, n):
     S = T.sem
     V, A, X, Y = g.vector, g.scalar, g.tensor, g.sync
-    mine, r = sides[h], h * NC + c
-    partner = sides[1 - h][c]
-    ba = 96 if h == 0 else 0
-    own = slice(h * HB, h * HB + HB)
+    r = h * NC + c
+    ba = 96 * h
+    at = 224 if h == 0 else 0
+    a0 = 128 * h
+    op = AluOpType
 
+    halves = slice(3, 1, -1) if c in (1, 2) else slice(2, 4)
     for i, q in ((0, Y), (1, A)):
-        q.dma_start(T.lst[16 * i:16 * i + 16, 0:4], T.sa[:]).then_inc(S.ll, 16)
-        q.dma_start(T.lst[16 * i:16 * i + 16, 4:16], T.sb[:]).then_inc(S.ll, 16)
-    Y.dma_start(T.abuf[:], T.a[:]).then_inc(S.la, 16)
-    Y.dma_start(T.bbuf[:], T.b[:]).then_inc(S.lb, 16)
+        q.dma_start(T.lst[16 * i:16 * i + 16, 1, 2:6], T.sa[:]).then_inc(S.ll, 16)
+        q.dma_start(T.lst[16 * i:16 * i + 16, halves, :], T.sb[:]).then_inc(S.ll, 16)
+    Y.dma_start(T.abuf[:, PAD:], T.a[:]).then_inc(S.la, 16)
+    Y.dma_start(T.bbuf[:, PAD:], T.b[:]).then_inc(S.lb, 16)
     for i in range(2):
-        A.dma_start(T.lq[16 * i:16 * i + 16, 0:24], T.pj[:]).then_inc(S.lp, 16)
-        A.dma_start(T.lq[16 * i:16 * i + 16, 24:32], T.pi[:]).then_inc(S.lp, 16)
+        Y.dma_start(T.lq[16 * i:16 * i + 16, 0:24], T.pj[:]).then_inc(S.lp, 16)
+        Y.dma_start(T.lq[16 * i:16 * i + 16, 24:32], T.pi[:]).then_inc(S.lp, 16)
 
-    V.memset(T.ta[:, (0 if h == 0 else 4 * 64):(4 * 96 if h == 0 else 4 * TW)], 0.0).then_inc(S.vz, 1)
+    V.memset(T.abuf[:, 0:PAD], 0.0).then_inc(S.vz, 1)
+    V.memset(T.bbuf[:, 0:PAD], 0.0).then_inc(S.vz, 1)
+    V.memset(T.ta[:, (4 * 64 if h == 0 else 0):(4 * TW if h == 0 else 4 * 96)], 0.0).then_inc(S.vz, 1)
+    V.memset(T.lst[0:32, 1, 0:2], 0).then_inc(S.vz, 1)
+    V.wait_ge(S.vz, 4)
     V.wait_ge(S.ll, 64)
-    for b in range(4):
-        V.tensor_scalar(T.l4[32 * b:32 * b + 32, :], T.lst[:], 4, 0, AluOpType.mult, AluOpType.max).then_inc(S.v1, 1)
-    V.wait_ge(S.v1, 4)
-    for t in range(4):
-        V.tensor_scalar(T.off[:, 16 * t:16 * t + 16], T.l4[:], t, None, AluOpType.add).then_inc(S.v2, 1)
-    V.wait_ge(S.v2, 4)
-    A.wait_ge(S.v2, 4)
-    V.wait_ge(S.la, 16)
-    A.wait_ge(S.la, 16)
+    for b in range(1, 4):
+        V.tensor_copy(T.lst[32 * b:32 * b + 32, 1:4, :], T.lst[0:32, 1:4, :]).then_inc(S.v1, 1)
+    V.wait_ge(S.v1, 3)
+    for t in (2, 3, 0, 1):
+        V.tensor_scalar(T.off[:, 18 * t:18 * t + 18], T.lst[:, 1:4, :], 4, PAD + t, op.mult, op.add).then_inc(S.v2 if t < 2 else S.v3, 1)
+    V.wait_ge(S.v2, 2)
+    A.wait_ge(S.v3, 2)
+    A.wait_ge(S.vz, 4)
+    for q in (V, A):
+        q.wait_ge(S.la, 16)
 
-    def pick(t, tile, first, n, win, o, sem):
-        out, in_ = tile[:, 4 * first + t:4 * (first + n):4], win[:, 0:1024].indirect(T.off[:, 16 * t + o:16 * t + o + n // 16])
+    def gather(t, tile, first, n, win, o, sem):
+        out, in_ = tile[:, 4 * first + t:4 * (first + n):4], win[:, 0:PAD + 1024].indirect(T.off[:, 18 * t + o:18 * t + o + n // 16])
         if t < 2:
             V.tensor_copy(out, in_).then_inc(sem, 1)
         else:
             A.activation(out, in_, COPY).then_inc(sem, 1)
 
     for t in range(4):
-        pick(t, T.ta, ba, 2 * CI, T.abuf, 0, S.gav if t < 2 else S.gas)
-    V.wait_ge(S.vz, 1)
+        gather(t, T.ta, ba, 2 * CI, T.abuf, 2, S.gav if t < 2 else S.gas)
     V.wait_ge(S.gav, 2)
     V.wait_ge(S.gas, 2)
-    V.quantize_mx(T.cac[:], T.cas[:], T.ta[:]).then_inc(S.qa, 1)
+    V.quantize_mx(T.ac[:, at:at + TW], T.cas[:], T.ta[:]).then_inc(S.qa, 1)
     V.wait_ge(S.lb, 16)
     A.wait_ge(S.lb, 16)
     for t in range(4):
-        pick(t, T.tb, 0, HB, T.bbuf, 4, S.gbv if t < 2 else S.gbs)
+        gather(t, T.tb, 0, HB, T.bbuf, 6, S.gbv if t < 2 else S.gbs)
     V.wait_ge(S.gbv, 2)
     V.wait_ge(S.gbs, 2)
-    V.quantize_mx(T.cbc[:], T.cbs[:], T.tb[:]).then_inc(S.qb, 1)
+    bt = (JW - CJ) * (1 - c % 2)
+    V.quantize_mx(T.bc[:, bt:bt + HB], T.bs[:, bt:bt + HB], T.tb[:]).then_inc(S.qb, 1)
 
-    Y.wait_ge(S.qb, 1)
-    Y.dma_start(T.lbc[:, r * CJ:r * CJ + CJ].bitcast(dt.uint8), T.cbc[:, c * CJ:c * CJ + CJ].bitcast(dt.uint8)).then_inc(S.oc, 16)
-    Y.dma_start(T.lbs[:, r * CJ:r * CJ + CJ], T.cbs[:, c * CJ:c * CJ + CJ]).then_inc(S.oc, 16)
+    done = [0]
 
-    fo, _fp, fs = forwarders(topo, me, mine)
-    _go, gp, gs = forwarders(topo, partner, sides[1 - h])
-    e1, e2, e3, e4 = a_plan(topo, me, fo, gp)
-    ls = len(e1) + len(e2) + len(e3) + len(e4)
-    g.wait_ge(S.qa, 1)
-    tr = []
-    for s, cx, cy, ex, ey in ((1 - h, gp, gs, e1, e2), (h, fo, fs, e3, e4)):
-        k = ba + CI * s
-        tr.append(move(topo, me, [cx], T.cac[:, k:k + CI].bitcast(dt.uint8), T.hxc[:].bitcast(dt.uint8), ex, S.hx))
-        tr.append(move(topo, me, [cy], T.cas[:, CI * s:CI * s + 128], T.hys[:, 128 * h:128 * h + 128], ey, S.hy))
-    g.remote_dma_fused(tr, local_sem=S.ls)
+    def step(*ins):
+        for i in ins:
+            i.then_inc(S.vx, 1)
+        done[0] += len(ins)
+        V.wait_ge(S.vx, done[0])
 
-    peers = [d for d in mine if d != me]
-    peers = [d for d in peers if not topo.mates(me, d) and not topo.same_plane(me, d)] + \
-            [d for d in peers if topo.mates(me, d) or topo.same_plane(me, d)]
-    off = topo.engines(me, peers[0])
-    g.wait_ge(S.qb, 1)
-    trc, trs = [], []
-    for i, d in enumerate(peers):
-        ec = off[0:4] if i == 0 else off[4 + 2 * i - 2:4 + 2 * i]
-        es = off[4:8] if i == 0 else off[2 * i - 2:2 * i]
-        k = mine.index(d)
-        trc.append(move(topo, me, [d], T.cbc[:, k * CJ:k * CJ + CJ].bitcast(dt.uint8), T.lbc[:, r * CJ:r * CJ + CJ].bitcast(dt.uint8), ec, S.b1c))
-        trs.append(move(topo, me, [d], T.cbs[:, k * CJ:k * CJ + CJ], T.lbs[:, r * CJ:r * CJ + CJ], es, S.b1s))
-    g.remote_dma_fused(trc, local_sem=S.ls)
-    g.remote_dma_fused(trs, local_sem=S.ls)
-    ls += 16
-
-    rid, pid = topo.addr(partner, me)
-    m = bits(topo.engines(me, partner))
-    g.wait_ge(S.oc, 32)
-    g.wait_ge(S.b1c, 8)
-    g.remote_dma(T.lbc[:, own].bitcast(dt.uint8), T.lbc[:, own].bitcast(dt.uint8), S.b2, S.ls, pid, rid, m)
-    g.wait_ge(S.b1s, 8)
-    g.remote_dma(T.lbs[:, own], T.lbs[:, own], S.b2, S.ls, pid, rid, m)
-    ls += 2 * len(topo.engines(me, partner))
-    g.wait_ge(S.ls, ls)
-
+    J, I = slice(0, 24), slice(24, 32)
+    hh, cc = (h, c) if c % 2 else (1 - h, c + 1)
     V.wait_ge(S.lp, 64)
-    V.tensor_scalar(T.k1[:], T.lq[:], 96, None, AluOpType.bitwise_and).then_inc(S.vx, 1)
-    V.tensor_scalar(T.k2[:], T.lq[:], 384, None, AluOpType.bitwise_and).then_inc(S.vx, 1)
-    V.wait_ge(S.vx, 2)
-    V.tensor_scalar(T.k3[:], T.k2[:], -0.75, None, AluOpType.mult).then_inc(S.vx, 1)
-    V.wait_ge(S.vx, 3)
-    V.tensor_tensor(T.k4[:], T.lq[:], T.k3[:], AluOpType.add).then_inc(S.vx, 1)
-    V.wait_ge(S.vx, 4)
-    V.tensor_tensor(T.k5[:], T.k4[:], T.k1[:], AluOpType.add).then_inc(S.vx, 1)
-    V.wait_ge(S.vx, 5)
-    V.tensor_tensor(T.ix[:, 0:24], T.k5[:, 0:24], T.k1[:, 0:24], AluOpType.add).then_inc(S.vx, 1)
-    for t in range(3):
-        for u in range(2):
-            V.tensor_scalar(T.ix[:, 24 + 2 * t + u:48:6], T.k5[:, 24 + u:32:2], 256 * t, None, AluOpType.add).then_inc(S.vx, 1)
-    V.wait_ge(S.vx, 12)
-    for b in range(4):
-        V.tensor_copy(T.ixu[32 * b:32 * b + 32, :], T.ix[:]).then_inc(S.vx, 1)
-    V.wait_ge(S.vx, 16)
-    A.wait_ge(S.vx, 16)
+    step(*[V.tensor_copy(T.lq[32 * b:32 * b + 32, :], T.lq[0:32, :]) for b in range(1, 4)])
+    step(V.tensor_scalar(T.k1[:, J], T.lq[:, J], HB, -HB, op.is_ge, op.mult),
+         V.tensor_scalar(T.k2[:, I], T.lq[:, I], CI * ((h - 1 - c) % NC), None, op.add),
+         V.tensor_scalar(T.k1[:, I], T.lq[:, I], 128, None, op.bitwise_and))
+    step(V.tensor_tensor(T.k3[:, J], T.k1[:, J], T.lq[:, J], op.add),
+         V.tensor_scalar(T.k4[:, J], T.k1[:, J], 2 * hh - 1, HB * hh - CJ * cc, op.mult, op.add),
+         V.tensor_scalar(T.k3[:, I], T.k1[:, I], -0.25, CI, op.mult, op.add))
+    step(V.tensor_scalar(T.k5[:, J], T.k3[:, J], CJ * cc, HB, op.is_lt, op.mult),
+         V.tensor_tensor(T.k6[:, J], T.k3[:, J], T.k4[:, J], op.add))
+    step(V.tensor_tensor(T.k2[:, J], T.k5[:, J], T.k6[:, J], op.add))
+    step(V.tensor_scalar(T.k4[:], T.k2[:], 96, None, op.bitwise_and),
+         V.tensor_scalar(T.k5[:], T.k2[:], 31, None, op.bitwise_and),
+         V.tensor_scalar(T.k1[:, J], T.k2[:, J], 384, None, op.bitwise_and))
+    step(*([V.tensor_scalar(T.k6[32 * b:32 * b + 32, J], T.k4[32 * b:32 * b + 32, J], -1, 32 * b + 128, op.mult, op.add) for b in range(4)]
+           + [V.tensor_scalar(T.k6[:, I], T.k4[:, I], 2, None, op.mult),
+              V.tensor_scalar(T.k3[:, J], T.k1[:, J], 0.25, None, op.mult)]))
+    step(V.tensor_scalar(T.k4[:, J], T.k6[:, J], 96, None, op.bitwise_and),
+         V.tensor_tensor(T.k1[:], T.k3[:], T.k5[:], op.add))
+    step(V.tensor_scalar(T.k6[:, J], T.k4[:, J], 3, None, op.mult))
+    step(V.tensor_tensor(T.k2[:], T.k1[:], T.k6[:], op.add))
+    step(*[V.tensor_scalar(T.ext[:, 24 * w + 2 * t + u:24 * w + 24:6], T.k2[:, 24 + u:32:2], 256 * t, None, op.add)
+           for w in range(2) for t in range(3) for u in range(2)])
+    step(*([V.tensor_copy(T.ixu[32 * a:32 * a + 32, 24:48], T.ext[32 * a:32 * a + 32, 6 * a:6 * a + 24]) for a in range(4)]
+           + [V.tensor_copy(T.ixu[:, J], T.k2[:, J])]))
+    A.wait_ge(S.vx, done[0])
 
-    e, l = (0, 1) if h == 0 else (2, 0)
-    X.wait_ge(S.oc, 32)
-    X.wait_ge(S.b1c, 8)
-    X.wait_ge(S.b1s, 8)
-    X.wait_ge(S.aa, 96)
-    for bank, t, x, w in ((0, e, 0, 256), (1, l, 0, 256), (2, l + 1, 0, 128), (3, l + 1, 128, 128)):
+    X.wait_ge(S.qa, 1)
+    X.wait_ge(S.qb, 1)
+    for sem in ("b1", "b2", "b3", "aa"):
+        X.wait_ge(S[sem], n[sem])
+    e = 0 if c % 2 else 2
+    for bank, t, x, w in ((0, e, 0, 256), (1, 1, 0, 256), (2, 2 - e, 0, 128), (3, 2 - e, 128, 128)):
+        k = b_run(c) + 128 * t
         if bank == 1:
-            X.wait_ge(S.b2, 2 * len(topo.engines(partner, me)))
-        X.matmul_mx(T.ps[:, 512 * bank:512 * bank + w], T.lbc[:, 128 * t:128 * t + 128], T.lbs[:, 128 * t:128 * t + 128],
-                    T.lac[:, x:x + w], T.las[:, x:x + w], True, True).then_inc(S["m%d" % bank], 1)
-        A_or_V = A.activation if bank in (0, 2) else V.tensor_copy
-        (A if bank in (0, 2) else V).wait_ge(S["m%d" % bank], 1)
+            X.wait_ge(S.bb, n["bb"])
+        X.matmul_mx(T.ps[:, 512 * bank:512 * bank + w], T.bc[:, k:k + 128], T.bs[:, k:k + 128],
+                    T.ac[:, a0 + x:a0 + x + w], T.las[:, x:x + w], True, True).then_inc(S["m%d" % bank], 1)
         args = (T.prod[:, 256 * t + x:256 * t + x + w], T.ps[:, 512 * bank:512 * bank + w])
-        (A_or_V(*args, COPY) if bank in (0, 2) else A_or_V(*args)).then_inc(S.cp, 1)
+        if bank in (0, 2):
+            A.wait_ge(S["m%d" % bank], 1)
+            A.activation(*args, COPY).then_inc(S.cp, 1)
+        else:
+            V.wait_ge(S["m%d" % bank], 1)
+            V.tensor_copy(*args).then_inc(S.cp, 1)
 
     for q in (V, A):
         q.wait_ge(S.cp, 4)
     win = T.prod[:, 0:768]
-    V.tensor_copy(T.pick1[:], win.indirect(T.ixu[:, 36:48])).then_inc(S.g1, 1)
-    A.activation(T.pick0[:], win.indirect(T.ixu[:, 24:36]), COPY).then_inc(S.g0, 1)
+    V.tensor_copy(T.pick[:, 192:384], win.indirect(T.ixu[:, 36:48])).then_inc(S.g1, 1)
+    A.activation(T.pick[:, 0:192], win.indirect(T.ixu[:, 24:36]), COPY).then_inc(S.g0, 1)
     V.wait_ge(S.g1, 1)
-    V.transpose(T.turned[:], T.pick1[:]).then_inc(S.tt, 1)
-    A.wait_ge(S.tt, 1)
+    V.transpose(T.turned[:, 96:192], T.pick[:, 288:384]).then_inc(S.t3, 1)
+    V.transpose(T.turned[:, 0:96], T.pick[:, 192:288]).then_inc(S.t2, 1)
     V.wait_ge(S.g0, 1)
-    for b in range(2):
-        for a in range(4):
-            V.transpose(T.fin[32 * b:32 * b + 32, 96 * a:96 * a + 96], T.pick0[32 * a:32 * a + 32, 96 * b:96 * b + 96]).then_inc(S.ft, 1)
-            A.activation(T.fin[32 * b + 64:32 * b + 96, 96 * a:96 * a + 96], T.turned[32 * a:32 * a + 32, 96 * b:96 * b + 96],
-                         COPY).then_inc(S.ft, 1)
+    A.wait_ge(S.t3, 1)
+    for a in range(4):
+        b1, b3 = 32 * ((a + 1) % 4), 32 * ((a + 3) % 4)
+        V.transpose(T.fin[b1:b1 + 32, 96:192], T.pick[32 * a:32 * a + 32, 96:192]).then_inc(S.ft, 1)
+        A.activation(T.fin[b3:b3 + 32, 288:384], T.turned[32 * a:32 * a + 32, 96:192], COPY).then_inc(S.ft, 1)
+    V.transpose(T.fin[:, 0:96], T.pick[:, 0:96]).then_inc(S.ft, 1)
+    A.wait_ge(S.t2, 1)
+    for a in (0, 64):
+        A.activation(T.fin[64 - a:128 - a, 192:288], T.turned[a:a + 64, 0:96], COPY).then_inc(S.ft, 1)
 
     for q in (V, A):
-        q.wait_ge(S.ft, 16)
-    V.tensor_copy(T.yout[:, 0:192], T.fin[:, 0:JW].indirect(T.ixu[:, 0:12])).then_inc(S.out, 1)
-    A.activation(T.yout[:, 192:JW], T.fin[:, 0:JW].indirect(T.ixu[:, 12:24]), COPY).then_inc(S.out, 1)
-    Y.wait_ge(S.out, 2)
-    Y.dma_start(T.y[:], T.yout[:]).then_inc(S.st, 16)
-    Y.wait_ge(S.st, 16)
+        q.wait_ge(S.ft, 11)
+    for w, sem in ((0, S.o0), (1, S.o1)):
+        k = 192 * w
+        V.tensor_copy(T.yout[:, k:k + 96], T.fin[:, 0:JW].indirect(T.ixu[:, 12 * w:12 * w + 6])).then_inc(sem, 1)
+        A.activation(T.yout[:, k + 96:k + 192], T.fin[:, 0:JW].indirect(T.ixu[:, 12 * w + 6:12 * w + 12]), COPY).then_inc(sem, 1)
+        Y.wait_ge(sem, 2)
+        Y.dma_start(T.y[:, k:k + 192], T.yout[:, k:k + 192]).then_inc(S.st, 16)
+    Y.wait_ge(S.st, 32)

@@ -3,15 +3,16 @@ from concourse.mybir import dt, AluOpType, ActivationFunctionType
 
 N, NC, CI, CJ, JW = 8, 4, 32, 48, 384
 HB = NC * CJ
-TW = 160
+TW = 128
 LB = HB - CJ
 PAD = 16
 
 SCRATCH = {
     "abuf": ("sbuf", [128, PAD + 1024], "bfloat16"),
     "bbuf": ("sbuf", [128, PAD + 1024], "bfloat16"),
-    "lst": ("sbuf", [128, 4, 6], "int32"),
-    "off": ("sbuf", [128, 72], "uint16"),
+    "lsa": ("sbuf", [128, 4], "int32"),
+    "lsb": ("sbuf", [128, 2, 6], "int32"),
+    "off": ("sbuf", [128, 64], "uint16"),
     "ta": ("sbuf", [128, 4 * TW], "bfloat16"),
     "tb": ("sbuf", [128, 4 * HB], "bfloat16"),
     "ac": ("sbuf", [128, 384], "float8_e4m3fn_x4"),
@@ -19,28 +20,31 @@ SCRATCH = {
     "las": ("sbuf", [128, 256], "uint8"),
     "bc": ("sbuf", [128, LB + JW], "float8_e4m3fn_x4"),
     "bs": ("sbuf", [128, LB + JW], "uint8"),
-    "hc": ("sbuf", [128, CJ], "float8_e4m3fn_x4"),
+    "hc": ("sbuf", [128, CI + CJ], "float8_e4m3fn_x4"),
     "hs": ("sbuf", [128, 256], "uint8"),
-    "ps": ("psum", [128, 2048], "float32"),
+    "ps": ("psum", [128, 3072], "float32"),
     "prod": ("sbuf", [128, 768], "float32"),
-    "pick": ("sbuf", [128, JW], "float32"),
-    "turned": ("sbuf", [128, 192], "float32"),
+    "pick": ("sbuf", [128, 3, 128], "float32"),
+    "turned": ("sbuf", [128, 96], "float32"),
     "fin": ("sbuf", [128, JW], "float32"),
     "yout": ("sbuf", [128, JW], "float32"),
-    "lq": ("sbuf", [128, 32], "int32"),
+    "lq": ("sbuf", [32, 32], "int32"),
     "k1": ("sbuf", [128, 32], "int32"),
     "k2": ("sbuf", [128, 32], "int32"),
     "k3": ("sbuf", [128, 32], "int32"),
     "k4": ("sbuf", [128, 32], "int32"),
     "k5": ("sbuf", [128, 32], "int32"),
     "k6": ("sbuf", [128, 32], "int32"),
-    "ext": ("sbuf", [128, 48], "int32"),
+    "ext": ("sbuf", [32, 16], "int32"),
+    "terms": ("sbuf", [32, N, 24], "int32"),
+    "sums": ("sbuf", [32, 4, 24], "int32"),
+    "quad": ("sbuf", [128, 2], "float32"),
     "ixu": ("sbuf", [128, 48], "uint16"),
 }
 CODES = ("ac", "bc", "hc")
-SEMAPHORES = ["la", "lb", "ll", "lp", "vz", "v1", "v2", "v3", "gav", "gas", "qa", "gbv", "gbs", "qb", "vx",
-              "hx", "aa", "b1", "b2", "b3", "bb", "ls", "m0", "m1", "m2", "m3",
-              "cp", "g0", "g1", "t2", "t3", "ft", "o0", "o1", "st"]
+SEMAPHORES = ["la", "lb", "ll", "lm", "lp", "vz", "v0", "v1", "v2", "v3", "v4", "gav", "gas", "qa", "gbv", "gbs", "qb", "vx",
+              "hx", "hy", "a0", "a1", "a2", "a3", "c0", "c1", "b2", "b4", "w0", "w1", "w2", "w3", "ls", "m0", "m1", "m2", "m3", "m4", "m5",
+              "p0", "p1", "p2", "g0", "g1", "t3", "ft", "o0", "o1", "st"]
 COPY = ActivationFunctionType.Copy
 
 
@@ -51,18 +55,29 @@ def helpers(topo, rank_core, side):
     return wide, [c for c in rest if c not in wide]
 
 
-def a_at(h, c, h2, c2):
-    return 64 * ((c2 - c - 1 + h) % NC) + CI * (1 - h2)
+def a_turn(topo, sides):
+    return [[c] + sorted((k for k in range(NC) if k != c), key=lambda k: not topo.mates(me, sides[0][k])) for c, me in enumerate(sides[0])]
+
+
+def a_at(turn, h, c, h2, c2):
+    i = turn[c].index(c2)
+    return 64 * (i if h else NC - 1 - i) + CI * (1 - h2)
 
 
 def b_run(c):
     return LB * (c % 2)
 
 
-def b_at(h, c, h2, c2):
-    if c % 2:
-        return LB + CJ * ((c2 - c) % NC) + HB * (h != h2)
-    return CJ * ((c2 - c - 1) % NC) + HB * (h == h2)
+def b_order(topo, sides):
+    order = []
+    for c, me in enumerate(sides[0]):
+        o = [c] + sorted((k for k in range(NC) if k != c), key=lambda k: topo.same_plane(me, sides[0][k]))
+        order.append(o if c % 2 else o[::-1])
+    return order
+
+
+def b_at(order, h, c, h2, c2):
+    return b_run(c) + CJ * order[c].index(c2) + HB * ((h != h2) if c % 2 else (h == h2))
 
 
 def b_tile(c, k):
@@ -70,24 +85,23 @@ def b_tile(c, k):
 
 
 def plan(topo, sides):
-    calls = {}
+    calls, order, turn = {}, b_order(topo, sides), a_turn(topo, sides)
     for h in range(2):
         for c in range(NC):
             me, mine, far_side = sides[h][c], sides[h], sides[1 - h]
             r, partner = h * NC + c, far_side[c]
-            (fo, fp, fs), narrow = helpers(topo, me, mine)
-            (_go, gp, gs), _ = helpers(topo, partner, far_side)
+            (fs, fp, fo), narrow = helpers(topo, me, mine)
+            (gs, gp, _go), (*_, gn) = helpers(topo, partner, far_side)
+            narrow = [narrow[0], narrow[-1]]
             off = topo.engines(me, partner)
             on = [e for e in topo.engines(me, fo) if e not in off]
             half = len(off) // 2
-            mate = [d for d in mine if topo.mates(me, d)][0]
             near = [k for k in range(NC) if topo.same_plane(me, mine[k])][0]
-            far = [mine.index(mate)] + [k for k in range(NC) if k not in (c, near) and mine[k] != mate]
-            pc, ca = narrow[0], narrow[2]
-            pd = helpers(topo, mate, mine)[1][3]
+            far = [k for k in range(NC) if k not in (c, near)]
+            ca, cb = narrow[-2:]
             peers = [k for k in range(NC) if k != c]
-            a0 = 128 * h
-            s0 = 224 if h == 0 else 96
+            a0 = 96 * h
+            s0 = 224 if h == 0 else 64
 
             def tile(k):
                 return b_tile(c, k)
@@ -95,31 +109,44 @@ def plan(topo, sides):
             own_run, far_run = (LB, LB + HB) if c % 2 else (HB, 0)
 
             def one(k, buf):
-                return [(mine[k], buf, b_at(h, k, h, c))]
+                return [(mine[k], buf, b_at(order, h, k, h, c))]
 
-            kd = NC - 1 - c
-            k1, k2 = [k for k in peers if k != kd]
+            def across(k, buf):
+                return [(far_side[k], buf, b_at(order, 1 - h, k, h, c))]
+
             kept = 2 * CJ * (c % 2)
             calls[me] = [
-                ("qa", [("ac", s0 + CI * (1 - h), CI, [(gp, "hc", 0)], off[:half], "hx"),
-                        ("cas", CI * (1 - h), 128, [(gs, "hs", 128 * (1 - h))], off[half:], "hx"),
-                        ("ac", s0 + CI * h, CI, [(fo, "hc", 0)], on[:half], "hx"),
-                        ("cas", CI * h, 128, [(fs, "hs", 128 * (1 - h))], on[half:], "hx")]),
-                ("qb", [("bc", tile(k1), CJ, one(k1, "bc"), off[:half], "b1"),
-                        ("bc", tile(k2), CJ, one(k2, "bc"), off[half:], "b1")]),
-                (None, [("bs", tile(k1), CJ, one(k1, "bs"), off[:half], "b2"),
-                        ("bs", tile(k2), CJ, one(k2, "bs"), off[half:], "b2")]),
-                (None, [("bs", tile(kd), CJ, one(kd, "bs"), off, "b2")]),
-                (None, [("bc", tile(kd), CJ, one(kd, "bc") + [(far_side[kd], "bc", b_at(1 - h, kd, h, c))], off, "b3")]),
-                (None, [("bc", tile(c), CJ, [(partner, "bc", b_at(1 - h, c, h, c))], off, "bb")]),
-                ("b1", [("bc", own_run + kept, 2 * CJ, [(partner, "bc", far_run + kept)], off, "bb")]),
-                ("b2", [("bs", own_run, HB, [(partner, "bs", far_run)], off, "bb")]),
+                ("qa", [("ac", s0 + CI * (1 - h), CI, [(gp, "hc", 0)], off, "hx"),
+                        ("ac", s0 + CI * h, CI, [(fo, "hc", 0)], on, "hx")]),
+                (None, [("cas", 64 * h + CI * (1 - h), CI, [(gs, "hs", CI * (1 - h))], off, "hx"),
+                        ("cas", 64 * h + CI * h, CI, [(fs, "hs", CI * (1 - h))], on, "hx")]),
+                (None, [("ac", s0 + CI * (1 - h), CI, [(gn, "hc", 0)], off, "hx"),
+                        ("ac", s0 + CI * h, CI, [(narrow[0], "hc", 0)], on, "hx")]),
+                ("qb", [("bc", tile(c), CJ, [(narrow[1], "hc", CI)], on, "hy")]),
+                (None, [("bs", tile(far[0]), CJ, one(far[0], "bs"), off[:half], "b2"),
+                        ("bs", tile(far[1]), CJ, one(far[1], "bs"), off[half:], "b2")]),
+                (None, [("bc", tile(near), CJ, [(fs, "hc", CI), (narrow[0], "hc", CI)], on, "hy")]),
+                (None, [("bs", tile(near), CJ, one(near, "bs"), off, "b2")]),
+                (None, [("bc", tile(far[0]), CJ, one(far[0], "bc") + across(far[0], "bc"), off[:half], "c%d" % h),
+                        ("bc", tile(far[1]), CJ, one(far[1], "bc") + across(far[1], "bc"), off[half:], "c%d" % h)]),
+                ("b2", [("bs", own_run, HB, [(partner, "bs", far_run)], off, "b4")]),
             ]
-            calls[fo] = [("hx", [("hc", 0, CI, [(mine[k], "ac", a0 + a_at(h, k, h, c)) for k in peers], off, "aa")])]
-            calls[fp] = [("hx", [("hc", 0, CI, [(mine[k], "ac", a0 + a_at(h, k, 1 - h, c)) for k in peers], off, "aa"),
-                                 ("hc", 0, CI, [(me, "ac", a0 + a_at(h, c, 1 - h, c))], on[:half], "aa")])]
-            calls[fs] = [("hx", [("hs", 96, 64, [(mine[k], "las", a_at(h, k, 1, c)) for k in peers], off, "aa"),
-                                 ("hs", 96, 64, [(me, "las", a_at(h, c, 1, c))], on[:half], "aa")])]
+            mate, last = turn[c][1], [k for k in far if k != turn[c][1]][0]
+
+            def codes(ks, h2, engines):
+                return ("hc", 0, CI, [(mine[k], "ac", a0 + a_at(turn, h, k, h2, c)) for k in ks], engines, "a%d" % c)
+
+            def planes(ks, engines):
+                return ("hs", 0, 64, [(mine[k], "las", a_at(turn, h, k, 1, c)) for k in ks], engines, "a%d" % c)
+
+            calls[fo] = [("hx", [codes([mate, last], h, off)])]
+            calls[fp] = [("hx", [codes([mate, last], 1 - h, off), codes([c], 1 - h, on)])]
+            calls[fs] = [("hx", [planes([mate, last, near], off), planes([c], on)])]
+            calls[narrow[0]] = [("hx", [codes([near], h, off)]),
+                                ("hy", [("hc", CI, CJ, across(near, "bc"), off, "b4")])]
+            calls[fs].append(("hy", [("hc", CI, CJ, one(near, "bc"), off, "b4")]))
+            calls[narrow[1]] = [("hx", [codes([near], 1 - h, off)]),
+                                ("hy", [("hc", CI, CJ, across(c, "bc"), off, "b4")])]
     return calls
 
 
@@ -153,25 +180,28 @@ def rank_program(g, core, T, topo):
     calls = plan(topo, sides)
     if T.rank_of(core) is not None:
         h = 0 if core in sides[0] else 1
-        rank_core(g, T, h, sides[h].index(core), {s: arrivals(calls, core, s) for s in ("aa", "b1", "b2", "b3", "bb")})
+        c = sides[h].index(core)
+        place = [a_at(a_turn(topo, sides), h, c, 0, k) - CI * k for k in range(NC)]
+        rank_core(g, T, h, c, b_order(topo, sides)[c], place, a_turn(topo, sides)[c], {s: arrivals(calls, core, s) for s in SEMAPHORES})
     if core in calls:
         issue(g, core, T, topo, calls)
 
 
-def rank_core(g, T, h, c, n):
+def rank_core(g, T, h, c, order, place, turn, n):
     S = T.sem
     V, A, X, Y = g.vector, g.scalar, g.tensor, g.sync
     r = h * NC + c
-    ba = 96 * h
+    ba = 64 * h
     at = 224 if h == 0 else 0
-    a0 = 128 * h
+    a0 = 96 * h
     op = AluOpType
 
-    halves = slice(3, 1, -1) if c in (1, 2) else slice(2, 4)
-    for i, q in ((0, Y), (1, A)):
-        q.dma_start(T.lst[16 * i:16 * i + 16, 1, 2:6], T.sa[:]).then_inc(S.ll, 16)
-        q.dma_start(T.lst[16 * i:16 * i + 16, halves, :], T.sb[:]).then_inc(S.ll, 16)
+    halves = slice(None, None, -1 if c in (1, 2) else 1)
+    for i in range(2):
+        (Y, A)[i % 2].dma_start(T.lsa[16 * i:16 * i + 16, :], T.sa[:]).then_inc(S.ll, 16)
     Y.dma_start(T.abuf[:, PAD:], T.a[:]).then_inc(S.la, 16)
+    for i, q in ((0, Y), (1, A)):
+        q.dma_start(T.lsb[16 * i:16 * i + 16, halves, :], T.sb[:]).then_inc(S.lm, 16)
     Y.dma_start(T.bbuf[:, PAD:], T.b[:]).then_inc(S.lb, 16)
     for i in range(2):
         Y.dma_start(T.lq[16 * i:16 * i + 16, 0:24], T.pj[:]).then_inc(S.lp, 16)
@@ -179,37 +209,45 @@ def rank_core(g, T, h, c, n):
 
     V.memset(T.abuf[:, 0:PAD], 0.0).then_inc(S.vz, 1)
     V.memset(T.bbuf[:, 0:PAD], 0.0).then_inc(S.vz, 1)
-    V.memset(T.ta[:, (4 * 64 if h == 0 else 0):(4 * TW if h == 0 else 4 * 96)], 0.0).then_inc(S.vz, 1)
-    V.memset(T.lst[0:32, 1, 0:2], 0).then_inc(S.vz, 1)
-    V.wait_ge(S.vz, 4)
-    V.wait_ge(S.ll, 64)
+    V.memset(T.ta[:, (4 * 64 if h == 0 else 0):(4 * TW if h == 0 else 4 * 64)], 0.0).then_inc(S.vz, 1)
+    for b in range(4):
+        for i in range(2):
+            V.memset(T.quad[32 * b:32 * b + 32, i:i + 1], float((32, 96)[i] * b)).then_inc(S.vz, 1)
+    V.wait_ge(S.vz, 11)
+    V.wait_ge(S.ll, 32)
     for b in range(1, 4):
-        V.tensor_copy(T.lst[32 * b:32 * b + 32, 1:4, :], T.lst[0:32, 1:4, :]).then_inc(S.v1, 1)
-    V.wait_ge(S.v1, 3)
-    for t in (2, 3, 0, 1):
-        V.tensor_scalar(T.off[:, 18 * t:18 * t + 18], T.lst[:, 1:4, :], 4, PAD + t, op.mult, op.add).then_inc(S.v2 if t < 2 else S.v3, 1)
-    V.wait_ge(S.v2, 2)
-    A.wait_ge(S.v3, 2)
-    A.wait_ge(S.vz, 4)
+        V.tensor_copy(T.lsa[32 * b:32 * b + 32], T.lsa[0:32]).then_inc(S.v0, 1)
+    V.wait_ge(S.v0, 3)
+    for t in (2, 0, 3, 1):
+        V.tensor_scalar(T.off[:, 16 * t:16 * t + 4], T.lsa[:], 4, PAD + t, op.mult, op.add).then_inc(S["w%d" % t], 1)
+    A.wait_ge(S.vz, 11)
     for q in (V, A):
         q.wait_ge(S.la, 16)
 
     def gather(t, tile, first, n, win, o, sem):
-        out, in_ = tile[:, 4 * first + t:4 * (first + n):4], win[:, 0:PAD + 1024].indirect(T.off[:, 18 * t + o:18 * t + o + n // 16])
+        out, in_ = tile[:, 4 * first + t:4 * (first + n):4], win[:, 0:PAD + 1024].indirect(T.off[:, 16 * t + o:16 * t + o + n // 16])
         if t < 2:
             V.tensor_copy(out, in_).then_inc(sem, 1)
         else:
             A.activation(out, in_, COPY).then_inc(sem, 1)
 
     for t in range(4):
-        gather(t, T.ta, ba, 2 * CI, T.abuf, 2, S.gav if t < 2 else S.gas)
+        (V if t < 2 else A).wait_ge(S["w%d" % t], 1)
+        gather(t, T.ta, ba, 2 * CI, T.abuf, 0, S.gav if t < 2 else S.gas)
+    V.wait_ge(S.lm, 32)
+    for b in range(1, 4):
+        V.tensor_copy(T.lsb[32 * b:32 * b + 32], T.lsb[0:32]).then_inc(S.v1, 1)
     V.wait_ge(S.gav, 2)
     V.wait_ge(S.gas, 2)
     V.quantize_mx(T.ac[:, at:at + TW], T.cas[:], T.ta[:]).then_inc(S.qa, 1)
+    V.wait_ge(S.v1, 3)
+    for t in (2, 0, 3, 1):
+        V.tensor_scalar(T.off[:, 16 * t + 4:16 * t + 16], T.lsb[:], 4, PAD + t, op.mult, op.add).then_inc(S["w%d" % t], 1)
     V.wait_ge(S.lb, 16)
     A.wait_ge(S.lb, 16)
     for t in range(4):
-        gather(t, T.tb, 0, HB, T.bbuf, 6, S.gbv if t < 2 else S.gbs)
+        (V if t < 2 else A).wait_ge(S["w%d" % t], 2)
+        gather(t, T.tb, 0, HB, T.bbuf, 4, S.gbv if t < 2 else S.gbs)
     V.wait_ge(S.gbv, 2)
     V.wait_ge(S.gbs, 2)
     bt = (JW - CJ) * (1 - c % 2)
@@ -224,71 +262,70 @@ def rank_core(g, T, h, c, n):
         V.wait_ge(S.vx, done[0])
 
     J, I = slice(0, 24), slice(24, 32)
-    hh, cc = (h, c) if c % 2 else (1 - h, c + 1)
+    hh = h if c % 2 else 1 - h
+    shift, q0 = [CJ * (order.index(q % NC) - q) + HB * (q // NC != hh) for q in range(N)], slice(0, 32)
+    ts, tt = V.tensor_scalar, V.tensor_tensor
     V.wait_ge(S.lp, 64)
-    step(*[V.tensor_copy(T.lq[32 * b:32 * b + 32, :], T.lq[0:32, :]) for b in range(1, 4)])
-    step(V.tensor_scalar(T.k1[:, J], T.lq[:, J], HB, -HB, op.is_ge, op.mult),
-         V.tensor_scalar(T.k2[:, I], T.lq[:, I], CI * ((h - 1 - c) % NC), None, op.add),
-         V.tensor_scalar(T.k1[:, I], T.lq[:, I], 128, None, op.bitwise_and))
-    step(V.tensor_tensor(T.k3[:, J], T.k1[:, J], T.lq[:, J], op.add),
-         V.tensor_scalar(T.k4[:, J], T.k1[:, J], 2 * hh - 1, HB * hh - CJ * cc, op.mult, op.add),
-         V.tensor_scalar(T.k3[:, I], T.k1[:, I], -0.25, CI, op.mult, op.add))
-    step(V.tensor_scalar(T.k5[:, J], T.k3[:, J], CJ * cc, HB, op.is_lt, op.mult),
-         V.tensor_tensor(T.k6[:, J], T.k3[:, J], T.k4[:, J], op.add))
-    step(V.tensor_tensor(T.k2[:, J], T.k5[:, J], T.k6[:, J], op.add))
-    step(V.tensor_scalar(T.k4[:], T.k2[:], 96, None, op.bitwise_and),
-         V.tensor_scalar(T.k5[:], T.k2[:], 31, None, op.bitwise_and),
-         V.tensor_scalar(T.k1[:, J], T.k2[:, J], 384, None, op.bitwise_and))
-    step(*([V.tensor_scalar(T.k6[32 * b:32 * b + 32, J], T.k4[32 * b:32 * b + 32, J], -1, 32 * b + 128, op.mult, op.add) for b in range(4)]
-           + [V.tensor_scalar(T.k6[:, I], T.k4[:, I], 2, None, op.mult),
-              V.tensor_scalar(T.k3[:, J], T.k1[:, J], 0.25, None, op.mult)]))
-    step(V.tensor_scalar(T.k4[:, J], T.k6[:, J], 96, None, op.bitwise_and),
-         V.tensor_tensor(T.k1[:], T.k3[:], T.k5[:], op.add))
-    step(V.tensor_scalar(T.k6[:, J], T.k4[:, J], 3, None, op.mult))
-    step(V.tensor_tensor(T.k2[:], T.k1[:], T.k6[:], op.add))
-    step(*[V.tensor_scalar(T.ext[:, 24 * w + 2 * t + u:24 * w + 24:6], T.k2[:, 24 + u:32:2], 256 * t, None, op.add)
-           for w in range(2) for t in range(3) for u in range(2)])
-    step(*([V.tensor_copy(T.ixu[32 * a:32 * a + 32, 24:48], T.ext[32 * a:32 * a + 32, 6 * a:6 * a + 24]) for a in range(4)]
-           + [V.tensor_copy(T.ixu[:, J], T.k2[:, J])]))
+    step(ts(T.terms[:, 0, :], T.lq[:, J], shift[0], None, op.add),
+         *[ts(T.terms[:, q, :], T.lq[:, J], CJ * q, shift[q] - shift[q - 1], op.is_ge, op.mult) for q in range(1, N)])
+    step(tt(T.sums[:], T.terms[:, 0:4, :], T.terms[:, 4:8, :], op.add),
+         ts(T.k1[q0, I], T.lq[:, I], 127, None, op.bitwise_and),
+         ts(T.k2[q0, I], T.lq[:, I], 128, -CI, op.is_ge, op.mult))
+    step(tt(T.terms[:, 0:2, :], T.sums[:, 0:2, :], T.sums[:, 2:4, :], op.add),
+         tt(T.k6[q0, I], T.k1[q0, I], T.k2[q0, I], op.add),
+         *[ts(o[q0, I], T.k1[q0, I], CI * k, place[k] - place[k - 1], op.is_ge, op.mult) for k, o in ((1, T.k3), (2, T.k4), (3, T.k5))])
+    step(*([tt(T.k1[32 * b:32 * b + 32, J], T.terms[:, 0, :], T.terms[:, 1, :], op.add) for b in range(4)]
+           + [tt(T.k1[q0, I], T.k3[q0, I], T.k4[q0, I], op.add), tt(T.k2[q0, I], T.k5[q0, I], T.k6[q0, I], op.add)]))
+    step(*([ts(T.k2[:, J], T.k1[:, J], 96, None, op.bitwise_and), ts(T.k3[:, J], T.k1[:, J], 384, None, op.bitwise_and)]
+           + [tt(T.k3[q0, I], T.k1[q0, I], T.k2[q0, I], op.add)]))
+    step(*([ts(T.k4[:, J], T.k2[:, J], T.quad[:, 0:1], JW, op.is_gt, op.mult),
+            ts(T.k5[:, J], T.k2[:, J], -4, T.quad[:, 1:2], op.mult, op.add),
+            ts(T.k6[:, J], T.k3[:, J], -0.75 if c % 2 else -1.25, 0 if c % 2 else 64, op.mult, op.add)]
+           + [ts(T.ext[:, 8 * w:8 * w + 8], T.k3[q0, I], place[0], None, op.add) for w in range(2)]))
+    step(tt(T.k2[:, J], T.k1[:, J], T.k4[:, J], op.add), tt(T.k3[:, J], T.k5[:, J], T.k6[:, J], op.add),
+         *[V.tensor_copy(T.ixu[32 * a:32 * a + 32, I], T.ext[:, 2 * a:2 * a + 8]) for a in range(4)])
+    step(tt(T.k4[:, J], T.k2[:, J], T.k3[:, J], op.add))
+    step(V.tensor_copy(T.ixu[:, J], T.k4[:, J]))
     A.wait_ge(S.vx, done[0])
 
     X.wait_ge(S.qa, 1)
     X.wait_ge(S.qb, 1)
-    for sem in ("b1", "b2", "b3", "aa"):
-        X.wait_ge(S[sem], n[sem])
-    e = 0 if c % 2 else 2
-    for bank, t, x, w in ((0, e, 0, 256), (1, 1, 0, 256), (2, 2 - e, 0, 128), (3, 2 - e, 128, 128)):
-        k = b_run(c) + 128 * t
-        if bank == 1:
-            X.wait_ge(S.bb, n["bb"])
+    waits = {0: ["b2", "c%d" % h] + ["a%d" % k for k in turn[:2]], 1: ["c%d" % (1 - h), "b4"], 3: ["a%d" % k for k in turn[2:]]}
+    for bank in range(6):
+        m, w = bank % 3, 128
+        x = 128 * (bank // 3 if h else 1 - bank // 3)
+        k = b_run(c) + 128 * (m if c % 2 else 2 - m)
+        for sem in waits.get(bank, ()):
+            X.wait_ge(S[sem], n[sem])
         X.matmul_mx(T.ps[:, 512 * bank:512 * bank + w], T.bc[:, k:k + 128], T.bs[:, k:k + 128],
                     T.ac[:, a0 + x:a0 + x + w], T.las[:, x:x + w], True, True).then_inc(S["m%d" % bank], 1)
-        args = (T.prod[:, 256 * t + x:256 * t + x + w], T.ps[:, 512 * bank:512 * bank + w])
-        if bank in (0, 2):
+        args = (T.prod[:, 256 * m + x:256 * m + x + w], T.ps[:, 512 * bank:512 * bank + w])
+        if bank % 2 == 0:
             A.wait_ge(S["m%d" % bank], 1)
-            A.activation(*args, COPY).then_inc(S.cp, 1)
+            A.activation(*args, COPY).then_inc(S["p%d" % m], 1)
         else:
             V.wait_ge(S["m%d" % bank], 1)
-            V.tensor_copy(*args).then_inc(S.cp, 1)
+            V.tensor_copy(*args).then_inc(S["p%d" % m], 1)
 
+    A.wait_ge(S.p0, 2)
+    A.activation(T.pick[:, 0, :], T.prod[:, 0:256].indirect(T.ixu[:, I]), COPY).then_inc(S.g1, 1)
+    V.wait_ge(S.p1, 2)
+    V.tensor_copy(T.pick[:, 1, :], T.prod[:, 256:512].indirect(T.ixu[:, I])).then_inc(S.g1, 1)
     for q in (V, A):
-        q.wait_ge(S.cp, 4)
-    win = T.prod[:, 0:768]
-    V.tensor_copy(T.pick[:, 192:384], win.indirect(T.ixu[:, 36:48])).then_inc(S.g1, 1)
-    A.activation(T.pick[:, 0:192], win.indirect(T.ixu[:, 24:36]), COPY).then_inc(S.g0, 1)
-    V.wait_ge(S.g1, 1)
-    V.transpose(T.turned[:, 96:192], T.pick[:, 288:384]).then_inc(S.t3, 1)
-    V.transpose(T.turned[:, 0:96], T.pick[:, 192:288]).then_inc(S.t2, 1)
+        q.wait_ge(S.p2, 2)
+    V.tensor_copy(T.pick[:, 2, 64:128], T.prod[:, 512:768].indirect(T.ixu[:, 28:32])).then_inc(S.g1, 1)
+    A.activation(T.pick[:, 2, 0:64], T.prod[:, 512:768].indirect(T.ixu[:, 24:28]), COPY).then_inc(S.g0, 1)
+    V.wait_ge(S.g1, 3)
+    V.transpose(T.turned[:], T.pick[:, :, 96:128]).then_inc(S.t3, 1)
+    for a in (0, 64):
+        V.transpose(T.fin[64 - a:128 - a, 192:288], T.pick[a:a + 64, :, 64:96]).then_inc(S.ft, 1)
     V.wait_ge(S.g0, 1)
     A.wait_ge(S.t3, 1)
     for a in range(4):
         b1, b3 = 32 * ((a + 1) % 4), 32 * ((a + 3) % 4)
-        V.transpose(T.fin[b1:b1 + 32, 96:192], T.pick[32 * a:32 * a + 32, 96:192]).then_inc(S.ft, 1)
-        A.activation(T.fin[b3:b3 + 32, 288:384], T.turned[32 * a:32 * a + 32, 96:192], COPY).then_inc(S.ft, 1)
-    V.transpose(T.fin[:, 0:96], T.pick[:, 0:96]).then_inc(S.ft, 1)
-    A.wait_ge(S.t2, 1)
-    for a in (0, 64):
-        A.activation(T.fin[64 - a:128 - a, 192:288], T.turned[a:a + 64, 0:96], COPY).then_inc(S.ft, 1)
+        V.transpose(T.fin[b1:b1 + 32, 96:192], T.pick[32 * a:32 * a + 32, :, 32:64]).then_inc(S.ft, 1)
+        A.activation(T.fin[b3:b3 + 32, 288:384], T.turned[32 * a:32 * a + 32, :], COPY).then_inc(S.ft, 1)
+    V.transpose(T.fin[:, 0:96], T.pick[:, :, 0:32]).then_inc(S.ft, 1)
 
     for q in (V, A):
         q.wait_ge(S.ft, 11)

from concourse.bass import DstId, RemoteDMATransfer
from concourse.mybir import dt, AluOpType, ActivationFunctionType

N, NC, CI, CJ, JW = 8, 4, 32, 48, 384
HB = NC * CJ
TW = 128
LB = HB - CJ
PAD = 16

SCRATCH = {
    "abuf": ("sbuf", [128, PAD + 1024], "bfloat16"),
    "bbuf": ("sbuf", [128, PAD + 1024], "bfloat16"),
    "lsa": ("sbuf", [128, 4], "int32"),
    "lsb": ("sbuf", [128, 2, 6], "int32"),
    "off": ("sbuf", [128, 64], "uint16"),
    "ta": ("sbuf", [128, 4 * TW], "bfloat16"),
    "tb": ("sbuf", [128, 4 * HB], "bfloat16"),
    "ac": ("sbuf", [128, 384], "float8_e4m3fn_x4"),
    "cas": ("sbuf", [128, TW], "uint8"),
    "las": ("sbuf", [128, 256], "uint8"),
    "bc": ("sbuf", [128, LB + JW], "float8_e4m3fn_x4"),
    "bs": ("sbuf", [128, LB + JW], "uint8"),
    "hc": ("sbuf", [128, CI + CJ], "float8_e4m3fn_x4"),
    "hs": ("sbuf", [128, 256], "uint8"),
    "ps": ("psum", [128, 3072], "float32"),
    "prod": ("sbuf", [128, 768], "float32"),
    "pick": ("sbuf", [128, 3, 128], "float32"),
    "turned": ("sbuf", [128, 96], "float32"),
    "fin": ("sbuf", [128, JW], "float32"),
    "yout": ("sbuf", [128, JW], "float32"),
    "lq": ("sbuf", [32, 32], "int32"),
    "k1": ("sbuf", [128, 32], "int32"),
    "k2": ("sbuf", [128, 32], "int32"),
    "k3": ("sbuf", [128, 32], "int32"),
    "k4": ("sbuf", [128, 32], "int32"),
    "k5": ("sbuf", [128, 32], "int32"),
    "k6": ("sbuf", [128, 32], "int32"),
    "ext": ("sbuf", [32, 16], "int32"),
    "terms": ("sbuf", [32, N, 24], "int32"),
    "sums": ("sbuf", [32, 4, 24], "int32"),
    "quad": ("sbuf", [128, 2], "float32"),
    "ixu": ("sbuf", [128, 48], "uint16"),
}
CODES = ("ac", "bc", "hc")
SEMAPHORES = ["la", "lb", "ll", "lm", "lp", "vz", "v0", "v1", "v2", "v3", "v4", "gav", "gas", "qa", "gbv", "gbs", "qb", "vx",
              "hx", "hy", "a0", "a1", "a2", "a3", "c0", "c1", "b2", "b4", "w0", "w1", "w2", "w3", "ls", "m0", "m1", "m2", "m3", "m4", "m5",
              "p0", "p1", "p2", "g0", "g1", "t3", "ft", "o0", "o1", "st"]
COPY = ActivationFunctionType.Copy


def helpers(topo, rank_core, side):
    rest = [c for c in topo.cores_of(rank_core) if c != rank_core]
    rest = [c for c in rest if topo.die(c) == topo.die(rank_core)] + [c for c in rest if topo.die(c) != topo.die(rank_core)]
    wide = [c for c in rest if all(topo.may_write(c, d) for d in side)]
    return wide, [c for c in rest if c not in wide]


def a_turn(topo, sides):
    return [[c] + sorted((k for k in range(NC) if k != c), key=lambda k: not topo.mates(me, sides[0][k])) for c, me in enumerate(sides[0])]


def a_at(turn, h, c, h2, c2):
    i = turn[c].index(c2)
    return 64 * (i if h else NC - 1 - i) + CI * (1 - h2)


def b_run(c):
    return LB * (c % 2)


def b_order(topo, sides):
    order = []
    for c, me in enumerate(sides[0]):
        o = [c] + sorted((k for k in range(NC) if k != c), key=lambda k: topo.same_plane(me, sides[0][k]))
        order.append(o if c % 2 else o[::-1])
    return order


def b_at(order, h, c, h2, c2):
    return b_run(c) + CJ * order[c].index(c2) + HB * ((h != h2) if c % 2 else (h == h2))


def b_tile(c, k):
    return (JW - CJ) * (1 - c % 2) + CJ * ((k + 2 * (c in (1, 2))) % NC)


def plan(topo, sides):
    calls, order, turn = {}, b_order(topo, sides), a_turn(topo, sides)
    for h in range(2):
        for c in range(NC):
            me, mine, far_side = sides[h][c], sides[h], sides[1 - h]
            r, partner = h * NC + c, far_side[c]
            (fs, fp, fo), narrow = helpers(topo, me, mine)
            (gs, gp, _go), (*_, gn) = helpers(topo, partner, far_side)
            narrow = [narrow[0], narrow[-1]]
            off = topo.engines(me, partner)
            on = [e for e in topo.engines(me, fo) if e not in off]
            half = len(off) // 2
            near = [k for k in range(NC) if topo.same_plane(me, mine[k])][0]
            far = [k for k in range(NC) if k not in (c, near)]
            ca, cb = narrow[-2:]
            peers = [k for k in range(NC) if k != c]
            a0 = 96 * h
            s0 = 224 if h == 0 else 64

            def tile(k):
                return b_tile(c, k)

            own_run, far_run = (LB, LB + HB) if c % 2 else (HB, 0)

            def one(k, buf):
                return [(mine[k], buf, b_at(order, h, k, h, c))]

            def across(k, buf):
                return [(far_side[k], buf, b_at(order, 1 - h, k, h, c))]

            kept = 2 * CJ * (c % 2)
            calls[me] = [
                ("qa", [("ac", s0 + CI * (1 - h), CI, [(gp, "hc", 0)], off, "hx"),
                        ("ac", s0 + CI * h, CI, [(fo, "hc", 0)], on, "hx")]),
                (None, [("cas", 64 * h + CI * (1 - h), CI, [(gs, "hs", CI * (1 - h))], off, "hx"),
                        ("cas", 64 * h + CI * h, CI, [(fs, "hs", CI * (1 - h))], on, "hx")]),
                (None, [("ac", s0 + CI * (1 - h), CI, [(gn, "hc", 0)], off, "hx"),
                        ("ac", s0 + CI * h, CI, [(narrow[0], "hc", 0)], on, "hx")]),
                ("qb", [("bc", tile(c), CJ, [(narrow[1], "hc", CI)], on, "hy")]),
                (None, [("bs", tile(far[0]), CJ, one(far[0], "bs"), off[:half], "b2"),
                        ("bs", tile(far[1]), CJ, one(far[1], "bs"), off[half:], "b2")]),
                (None, [("bc", tile(near), CJ, [(fs, "hc", CI), (narrow[0], "hc", CI)], on, "hy")]),
                (None, [("bs", tile(near), CJ, one(near, "bs"), off, "b2")]),
                (None, [("bc", tile(far[0]), CJ, one(far[0], "bc") + across(far[0], "bc"), off[:half], "c%d" % h),
                        ("bc", tile(far[1]), CJ, one(far[1], "bc") + across(far[1], "bc"), off[half:], "c%d" % h)]),
                ("b2", [("bs", own_run, HB, [(partner, "bs", far_run)], off, "b4")]),
            ]
            mate, last = turn[c][1], [k for k in far if k != turn[c][1]][0]

            def codes(ks, h2, engines):
                return ("hc", 0, CI, [(mine[k], "ac", a0 + a_at(turn, h, k, h2, c)) for k in ks], engines, "a%d" % c)

            def planes(ks, engines):
                return ("hs", 0, 64, [(mine[k], "las", a_at(turn, h, k, 1, c)) for k in ks], engines, "a%d" % c)

            calls[fo] = [("hx", [codes([mate, last], h, off)])]
            calls[fp] = [("hx", [codes([mate, last], 1 - h, off), codes([c], 1 - h, on)])]
            calls[fs] = [("hx", [planes([mate, last, near], off), planes([c], on)])]
            calls[narrow[0]] = [("hx", [codes([near], h, off)]),
                                ("hy", [("hc", CI, CJ, across(near, "bc"), off, "b4")])]
            calls[fs].append(("hy", [("hc", CI, CJ, one(near, "bc"), off, "b4")]))
            calls[narrow[1]] = [("hx", [codes([near], 1 - h, off)]),
                                ("hy", [("hc", CI, CJ, across(c, "bc"), off, "b4")])]
    return calls


def arrivals(calls, core, sem):
    return sum(len(t[4]) for cs in calls.values() for _w, ts in cs for t in ts for d in t[3] if d[0] == core and t[5] == sem)


def view(T, buf, a, n):
    v = T[buf][:, a:a + n]
    return v.bitcast(dt.uint8) if buf in CODES else v


def issue(g, core, T, topo, calls):
    sent = 0
    for wait, transfers in calls[core]:
        if wait is not None:
            g.wait_ge(T.sem[wait], arrivals(calls, core, wait) or 1)
        tr = []
        for buf, a, n, dsts, engines, sem in transfers:
            ids = [DstId(rid=topo.addr(d, core)[0], pnc=topo.addr(d, core)[1]) for d, _b, _a in dsts]
            tr.append(RemoteDMATransfer(dst_ids=ids, srcs=[view(T, buf, a, n)], dsts=[view(T, b, x, n) for _d, b, x in dsts],
                                        dma_engine_mask=sum(1 << e for e in engines), remote_sem=T.sem[sem]))
            sent += len(engines)
        g.remote_dma_fused(tr, local_sem=T.sem.ls)
    g.wait_ge(T.sem.ls, sent)


def rank_program(g, core, T, topo):
    cores = list(T.cores)
    sides = [[c for c in cores if topo.host(c) == topo.host(cores[0])], [c for c in cores if topo.host(c) != topo.host(cores[0])]]
    calls = plan(topo, sides)
    if T.rank_of(core) is not None:
        h = 0 if core in sides[0] else 1
        c = sides[h].index(core)
        place = [a_at(a_turn(topo, sides), h, c, 0, k) - CI * k for k in range(NC)]
        rank_core(g, T, h, c, b_order(topo, sides)[c], place, a_turn(topo, sides)[c], {s: arrivals(calls, core, s) for s in SEMAPHORES})
    if core in calls:
        issue(g, core, T, topo, calls)


def rank_core(g, T, h, c, order, place, turn, n):
    S = T.sem
    V, A, X, Y = g.vector, g.scalar, g.tensor, g.sync
    r = h * NC + c
    ba = 64 * h
    at = 224 if h == 0 else 0
    a0 = 96 * h
    op = AluOpType

    halves = slice(None, None, -1 if c in (1, 2) else 1)
    for i in range(2):
        (Y, A)[i % 2].dma_start(T.lsa[16 * i:16 * i + 16, :], T.sa[:]).then_inc(S.ll, 16)
    Y.dma_start(T.abuf[:, PAD:], T.a[:]).then_inc(S.la, 16)
    for i, q in ((0, Y), (1, A)):
        q.dma_start(T.lsb[16 * i:16 * i + 16, halves, :], T.sb[:]).then_inc(S.lm, 16)
    Y.dma_start(T.bbuf[:, PAD:], T.b[:]).then_inc(S.lb, 16)
    for i in range(2):
        Y.dma_start(T.lq[16 * i:16 * i + 16, 0:24], T.pj[:]).then_inc(S.lp, 16)
        Y.dma_start(T.lq[16 * i:16 * i + 16, 24:32], T.pi[:]).then_inc(S.lp, 16)

    V.memset(T.abuf[:, 0:PAD], 0.0).then_inc(S.vz, 1)
    V.memset(T.bbuf[:, 0:PAD], 0.0).then_inc(S.vz, 1)
    V.memset(T.ta[:, (4 * 64 if h == 0 else 0):(4 * TW if h == 0 else 4 * 64)], 0.0).then_inc(S.vz, 1)
    for b in range(4):
        for i in range(2):
            V.memset(T.quad[32 * b:32 * b + 32, i:i + 1], float((32, 96)[i] * b)).then_inc(S.vz, 1)
    V.wait_ge(S.vz, 11)
    V.wait_ge(S.ll, 32)
    for b in range(1, 4):
        V.tensor_copy(T.lsa[32 * b:32 * b + 32], T.lsa[0:32]).then_inc(S.v0, 1)
    V.wait_ge(S.v0, 3)
    for t in (2, 0, 3, 1):
        V.tensor_scalar(T.off[:, 16 * t:16 * t + 4], T.lsa[:], 4, PAD + t, op.mult, op.add).then_inc(S["w%d" % t], 1)
    A.wait_ge(S.vz, 11)
    for q in (V, A):
        q.wait_ge(S.la, 16)

    def gather(t, tile, first, n, win, o, sem):
        out, in_ = tile[:, 4 * first + t:4 * (first + n):4], win[:, 0:PAD + 1024].indirect(T.off[:, 16 * t + o:16 * t + o + n // 16])
        if t < 2:
            V.tensor_copy(out, in_).then_inc(sem, 1)
        else:
            A.activation(out, in_, COPY).then_inc(sem, 1)

    for t in range(4):
        (V if t < 2 else A).wait_ge(S["w%d" % t], 1)
        gather(t, T.ta, ba, 2 * CI, T.abuf, 0, S.gav if t < 2 else S.gas)
    V.wait_ge(S.lm, 32)
    for b in range(1, 4):
        V.tensor_copy(T.lsb[32 * b:32 * b + 32], T.lsb[0:32]).then_inc(S.v1, 1)
    V.wait_ge(S.gav, 2)
    V.wait_ge(S.gas, 2)
    V.quantize_mx(T.ac[:, at:at + TW], T.cas[:], T.ta[:]).then_inc(S.qa, 1)
    V.wait_ge(S.v1, 3)
    for t in (2, 0, 3, 1):
        V.tensor_scalar(T.off[:, 16 * t + 4:16 * t + 16], T.lsb[:], 4, PAD + t, op.mult, op.add).then_inc(S["w%d" % t], 1)
    V.wait_ge(S.lb, 16)
    A.wait_ge(S.lb, 16)
    for t in range(4):
        (V if t < 2 else A).wait_ge(S["w%d" % t], 2)
        gather(t, T.tb, 0, HB, T.bbuf, 4, S.gbv if t < 2 else S.gbs)
    V.wait_ge(S.gbv, 2)
    V.wait_ge(S.gbs, 2)
    bt = (JW - CJ) * (1 - c % 2)
    V.quantize_mx(T.bc[:, bt:bt + HB], T.bs[:, bt:bt + HB], T.tb[:]).then_inc(S.qb, 1)

    done = [0]

    def step(*ins):
        for i in ins:
            i.then_inc(S.vx, 1)
        done[0] += len(ins)
        V.wait_ge(S.vx, done[0])

    J, I = slice(0, 24), slice(24, 32)
    hh = h if c % 2 else 1 - h
    shift, q0 = [CJ * (order.index(q % NC) - q) + HB * (q // NC != hh) for q in range(N)], slice(0, 32)
    ts, tt = V.tensor_scalar, V.tensor_tensor
    V.wait_ge(S.lp, 64)
    step(ts(T.terms[:, 0, :], T.lq[:, J], shift[0], None, op.add),
         *[ts(T.terms[:, q, :], T.lq[:, J], CJ * q, shift[q] - shift[q - 1], op.is_ge, op.mult) for q in range(1, N)])
    step(tt(T.sums[:], T.terms[:, 0:4, :], T.terms[:, 4:8, :], op.add),
         ts(T.k1[q0, I], T.lq[:, I], 127, None, op.bitwise_and),
         ts(T.k2[q0, I], T.lq[:, I], 128, -CI, op.is_ge, op.mult))
    step(tt(T.terms[:, 0:2, :], T.sums[:, 0:2, :], T.sums[:, 2:4, :], op.add),
         tt(T.k6[q0, I], T.k1[q0, I], T.k2[q0, I], op.add),
         *[ts(o[q0, I], T.k1[q0, I], CI * k, place[k] - place[k - 1], op.is_ge, op.mult) for k, o in ((1, T.k3), (2, T.k4), (3, T.k5))])
    step(*([tt(T.k1[32 * b:32 * b + 32, J], T.terms[:, 0, :], T.terms[:, 1, :], op.add) for b in range(4)]
           + [tt(T.k1[q0, I], T.k3[q0, I], T.k4[q0, I], op.add), tt(T.k2[q0, I], T.k5[q0, I], T.k6[q0, I], op.add)]))
    step(*([ts(T.k2[:, J], T.k1[:, J], 96, None, op.bitwise_and), ts(T.k3[:, J], T.k1[:, J], 384, None, op.bitwise_and)]
           + [tt(T.k3[q0, I], T.k1[q0, I], T.k2[q0, I], op.add)]))
    step(*([ts(T.k4[:, J], T.k2[:, J], T.quad[:, 0:1], JW, op.is_gt, op.mult),
            ts(T.k5[:, J], T.k2[:, J], -4, T.quad[:, 1:2], op.mult, op.add),
            ts(T.k6[:, J], T.k3[:, J], -0.75 if c % 2 else -1.25, 0 if c % 2 else 64, op.mult, op.add)]
           + [ts(T.ext[:, 8 * w:8 * w + 8], T.k3[q0, I], place[0], None, op.add) for w in range(2)]))
    step(tt(T.k2[:, J], T.k1[:, J], T.k4[:, J], op.add), tt(T.k3[:, J], T.k5[:, J], T.k6[:, J], op.add),
         *[V.tensor_copy(T.ixu[32 * a:32 * a + 32, I], T.ext[:, 2 * a:2 * a + 8]) for a in range(4)])
    step(tt(T.k4[:, J], T.k2[:, J], T.k3[:, J], op.add))
    step(V.tensor_copy(T.ixu[:, J], T.k4[:, J]))
    A.wait_ge(S.vx, done[0])

    X.wait_ge(S.qa, 1)
    X.wait_ge(S.qb, 1)
    waits = {0: ["b2", "c%d" % h] + ["a%d" % k for k in turn[:2]], 1: ["c%d" % (1 - h), "b4"], 3: ["a%d" % k for k in turn[2:]]}
    for bank in range(6):
        m, w = bank % 3, 128
        x = 128 * (bank // 3 if h else 1 - bank // 3)
        k = b_run(c) + 128 * (m if c % 2 else 2 - m)
        for sem in waits.get(bank, ()):
            X.wait_ge(S[sem], n[sem])
        X.matmul_mx(T.ps[:, 512 * bank:512 * bank + w], T.bc[:, k:k + 128], T.bs[:, k:k + 128],
                    T.ac[:, a0 + x:a0 + x + w], T.las[:, x:x + w], True, True).then_inc(S["m%d" % bank], 1)
        args = (T.prod[:, 256 * m + x:256 * m + x + w], T.ps[:, 512 * bank:512 * bank + w])
        if bank % 2 == 0:
            A.wait_ge(S["m%d" % bank], 1)
            A.activation(*args, COPY).then_inc(S["p%d" % m], 1)
        else:
            V.wait_ge(S["m%d" % bank], 1)
            V.tensor_copy(*args).then_inc(S["p%d" % m], 1)

    A.wait_ge(S.p0, 2)
    A.activation(T.pick[:, 0, :], T.prod[:, 0:256].indirect(T.ixu[:, I]), COPY).then_inc(S.g1, 1)
    V.wait_ge(S.p1, 2)
    V.tensor_copy(T.pick[:, 1, :], T.prod[:, 256:512].indirect(T.ixu[:, I])).then_inc(S.g1, 1)
    for q in (V, A):
        q.wait_ge(S.p2, 2)
    V.tensor_copy(T.pick[:, 2, 64:128], T.prod[:, 512:768].indirect(T.ixu[:, 28:32])).then_inc(S.g1, 1)
    A.activation(T.pick[:, 2, 0:64], T.prod[:, 512:768].indirect(T.ixu[:, 24:28]), COPY).then_inc(S.g0, 1)
    V.wait_ge(S.g1, 3)
    V.transpose(T.turned[:], T.pick[:, :, 96:128]).then_inc(S.t3, 1)
    for a in (0, 64):
        V.transpose(T.fin[64 - a:128 - a, 192:288], T.pick[a:a + 64, :, 64:96]).then_inc(S.ft, 1)
    V.wait_ge(S.g0, 1)
    A.wait_ge(S.t3, 1)
    for a in range(4):
        b1, b3 = 32 * ((a + 1) % 4), 32 * ((a + 3) % 4)
        V.transpose(T.fin[b1:b1 + 32, 96:192], T.pick[32 * a:32 * a + 32, :, 32:64]).then_inc(S.ft, 1)
        A.activation(T.fin[b3:b3 + 32, 288:384], T.turned[32 * a:32 * a + 32, :], COPY).then_inc(S.ft, 1)
    V.transpose(T.fin[:, 0:96], T.pick[:, :, 0:32]).then_inc(S.ft, 1)

    for q in (V, A):
        q.wait_ge(S.ft, 11)
    for w, sem in ((0, S.o0), (1, S.o1)):
        k = 192 * w
        V.tensor_copy(T.yout[:, k:k + 96], T.fin[:, 0:JW].indirect(T.ixu[:, 12 * w:12 * w + 6])).then_inc(sem, 1)
        A.activation(T.yout[:, k + 96:k + 192], T.fin[:, 0:JW].indirect(T.ixu[:, 12 * w + 6:12 * w + 12]), COPY).then_inc(sem, 1)
        Y.wait_ge(sem, 2)
        Y.dma_start(T.y[:, k:k + 192], T.yout[:, k:k + 192]).then_inc(S.st, 16)
    Y.wait_ge(S.st, 32)
